import numpy as np, ml_dtypes
CORES = [8,9,10,11,12,13]
N = 6
import mx_ref
BF = ml_dtypes.bfloat16
def cols(t, e):
    v = np.concatenate([t.reshape(128, -1, 4), np.zeros((128, 1, 4), BF)], axis=1)
    return np.ascontiguousarray(v[:, e]).reshape(128, -1)
def decode(q):
    o = []
    for b in range(4):
        e = np.zeros((128, 128, 4), np.float32); e[np.arange(128), np.arange(128), b] = 1
        o.append(mx_ref.matmul(mx_ref.quantize(e.reshape(128, 512).astype(BF)), q))
    return np.stack(o, axis=2).reshape(128, -1)
def f(rng, *shape):
    return mx_ref.flush((rng.standard_normal(shape, dtype=np.float32) * np.exp2(rng.integers(-2, 3, shape[:-1] + (1,)))).astype(BF))
def wide(rng, *shape, cols=0):
    v = rng.standard_normal(shape, dtype=np.float32) * np.exp2(rng.integers(-12, 13, shape)).astype(np.float32)
    if cols: v *= np.repeat(np.exp2(rng.integers(-cols, cols + 1, shape[:-2] + (1, shape[-1] // 4))) * (rng.random(shape[:-2] + (1, shape[-1] // 4)) > 0.0625), 4, axis=-1).astype(np.float32)
    return mx_ref.flush(v.astype(BF))
K = 512
def plant(t, k, v):
    o = t.astype(np.float32).reshape(128, -1, 4); o[:, k] = v
    return o.reshape(128, -1).astype(BF)
def setup_inputs(rng):
    return {"x": f(rng, N, 128, 512), "c1": f(rng, N, 128, 4 * K), "c2": f(rng, N, 128, 4 * K)}
def setup_inputs_last(rng):
    d = setup_inputs(rng); u = f(rng, 128, 4).astype(np.float32).reshape(128, 1, 4); x = []
    s = np.exp2(np.where(np.arange(128) < 120, 2, 0) + np.arange(128) % 2).astype(np.float32).reshape(1, 128, 1)
    for r in range(N):
        x.append(plant(d["x"][r], rng.permutation(128), u * s))
    d["x"] = np.stack(x)
    for c in ("c1", "c2"):
        d[c] = np.stack([plant(d[c][q], [K - 1], np.float32(2) * u) if q == N - 1 else d[c][q] for q in range(N)])
    return d
def setup_inputs_negative(rng):
    d = setup_inputs(rng)
    for c, s in (("x", 1), ("c1", -1), ("c2", -1)):
        d[c] = (np.abs(d[c].astype(np.float32)) * np.float32(s * 2.0 ** 20)).astype(BF)
    return d
def setup_inputs_own(rng):
    d = setup_inputs(rng)
    for c, s in (("c1", 2), ("c2", -2)):
        d[c] = np.stack([plant(d[c][r], rng.permutation(K)[:128], np.float32(s) * d["x"][r].astype(np.float32).reshape(128, -1, 4)) for r in range(N)])
    return d
def setup_inputs_spread(rng):
    d = setup_inputs(rng); d["x"] = wide(rng, N, 128, 512, cols=8)
    for c in ("c1", "c2"): d[c] = wide(rng, N, 128, 4 * K, cols=2)
    return d
def setup_inputs_ties(rng):
    d = setup_inputs(rng)
    d["x"] = np.stack([plant(d["x"][r], rng.permutation(128)[:1], np.zeros((128, 1, 4), np.float32)) for r in range(N)])
    for c in ("c1", "c2"):
        a = f(rng, N, 128, K)
        d[c] = np.stack([cols(np.concatenate([a[q], a[q], a[(q + 1) % N], a[(q + 2) % N]], axis=1), rng.permutation(K)) for q in range(N)])
    return d
def check_inputs(d):
    b = []
    for c in ("x", "c1", "c2"):
        a = np.abs(d[c].astype(np.float32))
        if not (np.isfinite(a) & ((a == 0) | ((a >= 2.0 ** -30) & (a <= 2.0 ** 30)))).all(): b.append(c)
    return b
def winners(v, book):
    s = np.concatenate([mx_ref.matmul(v, q) for q in book], axis=1)
    w = np.argmax(s + np.float32(0), axis=1)
    return w, s[np.arange(128), w]
def chosen(t, e):
    return t.reshape(128, -1, 4)[:, e].reshape(128, -1)
def reference(x, c1, c2):
    q1 = [mx_ref.quantize(c1[q]) for q in range(N)]
    q2 = [mx_ref.quantize(c2[q]) for q in range(N)]
    d1 = np.concatenate([decode(q) for q in q1], axis=1)
    d2 = np.concatenate([decode(q) for q in q2], axis=1)
    y = np.zeros((N, 128, 512), np.float32); no = np.zeros((N, 4, 128), np.float32)
    for r in range(N):
        w1, s1 = winners(mx_ref.quantize(x[r]), q1)
        R = (x[r].astype(np.float32) - chosen(d1, w1)).astype(BF)
        w2, s2 = winners(mx_ref.quantize(R), q2)
        y[r] = R.astype(np.float32) - chosen(d2, w2)
        no[r, 0] = w1; no[r, 1] = w2; no[r, 2] = s1; no[r, 3] = s2
    return {"y": y, "no": no}

@@ -1,0 +1,450 @@
+from concourse.bass import DstId, RemoteDMATransfer
+from concourse.mybir import dt, AluOpType, AxisListType, ActivationFunctionType
+
+N = 6
+K = 512
+A = AluOpType
+F = ActivationFunctionType
+
+SCRATCH = {
+    "xt": ("sbuf", [128, 512], "bfloat16"),
+    "xsw": ("sbuf", [128, 512], "bfloat16"),
+    "rt": ("sbuf", [128, 512], "bfloat16"),
+    "rsw": ("sbuf", [128, 512], "bfloat16"),
+    "yt": ("sbuf", [128, 512], "float32"),
+    "neg": ("sbuf", [128, 512], "float32"),
+    "ones": ("sbuf", [128, 516], "bfloat16"),
+    "zt": ("sbuf", [128, 516], "bfloat16"),
+    "eq": ("sbuf", [128, 512], "float8_e4m3fn_x4"),
+    "ep": ("sbuf", [128, 512], "uint8"),
+    "bm": ("sbuf", [128, 32], "float32"),
+    "mask": ("sbuf", [128, 32], "float32"),
+    "pi": ("sbuf", [128, 8], "int32"),
+    "p3": ("sbuf", [128, 8], "int32"),
+    "acol": ("sbuf", [128, 8], "float32"),
+    "a768": ("sbuf", [128, 8], "float32"),
+    "nc": ("sbuf", [128, 8], "float32"),
+    "wt": ("sbuf", [128, 8], "float32"),
+    "q512": ("sbuf", [128, 8], "float32"),
+    "lx": ("sbuf", [128, 14, 32], "float32"),
+    "lt": ("sbuf", [128, 14, 32], "float32"),
+    "ly": ("sbuf", [128, 14, 16], "float32"),
+    "ls": ("sbuf", [128, 14, 16], "float32"),
+    "lf": ("sbuf", [128, 14, 32], "float32"),
+    "off": ("sbuf", [128, 14, 32], "uint16"),
+    "sb": ("psum", [128, 2048], "float32"),
+    "up": ("psum", [128, 2048], "float32"),
+}
+for _s in (1, 2):
+    SCRATCH["ct%d" % _s] = ("sbuf", [128, 4 * K], "bfloat16")
+    SCRATCH["cq%d" % _s] = ("sbuf", [128, K], "float8_e4m3fn_x4")
+    SCRATCH["cp%d" % _s] = ("sbuf", [128, K], "uint8")
+    SCRATCH["xq%d" % _s] = ("sbuf", [128, 128 * N], "float8_e4m3fn_x4")
+    SCRATCH["xp%d" % _s] = ("sbuf", [128, 128 * N], "uint8")
+    SCRATCH["wq%d" % _s] = ("sbuf", [128, 128 * N], "float8_e4m3fn_x4")
+    SCRATCH["wp%d" % _s] = ("sbuf", [128, 128 * N], "uint8")
+    SCRATCH["win%d" % _s] = ("sbuf", [128, 512 * N], "bfloat16")
+    SCRATCH["sc%d" % _s] = ("sbuf", [128, 4 * N], "float32")
+    SCRATCH["dc%d" % _s] = ("sbuf", [128, 40], "float32")
+    for _r in range(N):
+        SCRATCH["rm%d_%d" % (_s, _r)] = ("sbuf", [128, 516], "float32")
+        SCRATCH["jk%d_%d" % (_s, _r)] = ("sbuf", [128, 512], "bfloat16")
+        SCRATCH["gt%d_%d" % (_s, _r)] = ("sbuf", [128, 512], "bfloat16")
+        SCRATCH["oq%d_%d" % (_s, _r)] = ("sbuf", [128, 128], "float8_e4m3fn_x4")
+        SCRATCH["op%d_%d" % (_s, _r)] = ("sbuf", [128, 128], "uint8")
+
+SEMAPHORES = ["cv", "cs", "cp", "cg", "sent", "ld_x", "ld_xs", "ld_c1", "ld_c2", "ld_rs", "st_no", "st_y0", "st_y1"]
+for _s in (1, 2):
+    SEMAPHORES += ["pair%d" % _s]
+    for _r in range(N):
+        SEMAPHORES += ["xa%d_%d" % (_s, _r), "wa%d_%d" % (_s, _r)]
+
+CSEM = {"V": "cv", "S": "cs", "P": "cp", "G": "cg"}
+GROUPS = {1: [[0, 1], [2, 3], [4, 5]], 2: [[0, 1], [2, 3], [4, 5]]}
+EST = {"v0": 0.0, "v": 0.00104, "s0": 0.03, "s": 0.00104, "sg": 0.0019, "mm": 0.00095, "g0": 0.16, "g": 0.0018,
+       "wake": 0.08, "rem": 0.25, "hop": 2.2, "hopx": 3.0, "dma": 2.0, "dmai": 0.08, "bias": 0.25, "alt": 2.0}
+SWAP = (0, 2, 1, 3)
+_memo = {}
+
+
+def build(topo, cores, E):
+    ops = []
+    now = [0]
+    got = {}
+    sent = {}
+    arr = []
+    R = range(N)
+
+    def op(c, q, dur, deps, emit, kind="c", sem=None, lat=0.0):
+        ops.append({"c": c, "q": q, "dur": dur, "deps": [d for d in deps if d is not None], "emit": emit, "kind": kind,
+                    "sem": sem, "lat": lat, "bias": E["bias"] * now[0]})
+        return len(ops) - 1
+
+    def V(c, n, deps, emit, fast=False):
+        return op(c, "V", E["v0"] + max(64, n * (0.5 if fast else 1)) * E["v"], deps, emit)
+
+    def S(c, n, deps, emit):
+        return op(c, "S", E["s0"] + max(64, n) * E["s"], deps, emit)
+
+    def X(c, n, deps, ev, es, ind=False):
+        i = op(c, "V", 0.0, deps, None)
+        dv, ds = E["v0"] + max(64, n) * E["v"], E["s0"] + max(64, n) * E["s"]
+        if ind:
+            dv, ds = 0.05 + n * E["sg"], 0.065 + n * E["sg"]
+        ops[i]["alt"] = {"V": (dv, ev), "S": (ds, es)}
+        ops[i]["dur"] = min(dv, ds)
+        return i
+
+    def G(c, n, deps, emit):
+        return op(c, "G", E["g0"] + n * E["g"], deps, emit)
+
+    def MM(c, n, deps, emit):
+        return op(c, "P", (n + 16) * E["mm"], deps, emit)
+
+    def D(c, q, deps, emit, sem, total=16, more=0.0):
+        return op(c, q, E["dmai"], deps, emit, "d", (sem, total), E["dma"] + more)
+
+    def QZ(c, n, deps, emit):
+        return op(c, "V", 0.015 + 4 * n * 0.00028, deps, emit)
+
+    def send(c, parts, deps):
+        share = 1
+        while share < len(parts):
+            share *= 2
+
+        def emit(g, T):
+            ts = []
+            for i, (dst, sem, src, land) in enumerate(parts):
+                eng = topo.engines(cores[c], cores[dst[0]])
+                w = len(eng) // share
+                m = 0
+                for e in eng[i * w:(i + 1) * w]:
+                    m |= 1 << e
+                ids = []
+                for d in dst:
+                    rid, pid, _ = topo.addr(cores[d])
+                    ids.append(DstId(rid=rid, pnc=pid))
+                ts.append(RemoteDMATransfer(dst_ids=ids, dma_engine_mask=m, remote_sem=T.sem[sem], srcs=[src(T)], dsts=[land(T) for _ in dst], alu_op=0))
+            return g.remote_dma_fused(ts, local_sem=T.sem.sent)
+        for dst, sem, _, _ in parts:
+            w = len(topo.engines(cores[c], cores[dst[0]])) // share
+            for d in dst:
+                got[(d, sem)] = got.get((d, sem), 0) + w
+            sent[c] = sent.get(c, 0) + w
+        return op(c, "G", E["rem"] + 0.06 * (len(parts) - 1), deps, emit, "r")
+
+    def arrive(c, sem, deps, lat):
+        o = op(c, None, 0.0, deps, None, "a", (sem, None), lat)
+        arr.append(o)
+        return o
+
+    st = [{} for _ in R]
+    for c in R:
+        s = st[c]
+        s["ldx"] = D(c, "Y", [], lambda g, T: g.sync.dma_start(T.xt[:], T.x[:]), "ld_x")
+        s["ldc1"] = D(c, "Y", [], lambda g, T: g.sync.dma_start(T.ct1[:], T.c1[:]), "ld_c1", 16, 1.2)
+        s["qx1"] = QZ(c, 128, [s["ldx"]], lambda g, T, c=c: g.vector.quantize_mx(T.xq1[:, 128 * c:128 * c + 128], T.xp1[:, 128 * c:128 * c + 128], T.xt[:]))
+        s["neg"] = V(c, 512, [], lambda g, T: g.vector.memset(T.neg[:], -1e29))
+        s["ones"] = V(c, 516, [], lambda g, T: g.vector.memset(T.ones[:], 1.0), True)
+        pi = G(c, 1, [], lambda g, T: g.iota(T.pi[:, 0:1], [[0, 1]], 0, 1))
+        bm = G(c, 32, [], lambda g, T: g.iota(T.bm[:], [[0, 2], [1, 4], [0, 4]], 0, 0, allow_small_or_imprecise_dtypes=True))
+        p3 = V(c, 1, [pi], lambda g, T: g.vector.tensor_scalar(T.p3[:, 0:1], T.pi[:, 0:1], 3, None, A.bitwise_and))
+        s["acol"] = V(c, 1, [p3], lambda g, T: g.vector.tensor_copy(T.acol[:, 0:1], T.p3[:, 0:1]))
+        s["mask"] = V(c, 32, [bm, s["acol"]], lambda g, T: g.vector.tensor_scalar(T.mask[:], T.bm[:], T.acol[:, 0:1], None, A.is_equal))
+        s["a768"] = V(c, 1, [s["acol"]], lambda g, T: g.vector.tensor_scalar(T.a768[:, 0:1], T.acol[:, 0:1], 128.0 * N, None, A.mult))
+        s["qc1"] = QZ(c, 512, [s["ldc1"]], lambda g, T: g.vector.quantize_mx(T.cq1[:], T.cp1[:], T.ct1[:]))
+
+    def spread(c, stage, q):
+        dst = [d for d in R if d != c]
+        sem = "xa%d_%d" % (stage, c)
+        a, b = 128 * c, 128 * c + 128
+        vq = lambda T: T["xq%d" % stage][:, a:b].bitcast(dt.uint8)
+        vp = lambda T: T["xp%d" % stage][:, a:b]
+        s1 = send(c, [(dst, sem, vq, vq)], [q])
+        s2 = send(c, [(dst, sem, vp, vp)], [q])
+        for d in dst:
+            st[d]["x%d_%d" % (stage, c)] = arrive(d, sem, [s1, s2], E["hopx"])
+        st[c]["x%d_%d" % (stage, c)] = q
+
+    for c in R:
+        s = st[c]
+        spread(c, 1, s["qx1"])
+        s["zt"] = G(c, 516, [s["ones"]], lambda g, T: g.affine_select(T.zt[:], T.ones[:], [[-1, 516]], A.is_equal, 0.0, 4, 4))
+        p0 = G(c, 1, [], lambda g, T: g.iota(T.nc[:, 0:1], [[0, 1]], 1024, 1, allow_small_or_imprecise_dtypes=True))
+        s["nc"] = [V(c, 1, [p0], lambda g, T, k=k: g.vector.tensor_scalar(T.nc[32 * k:32 * k + 32, 1:2], T.nc[32 * k:32 * k + 32, 0:1], 32.0 * (SWAP[k] - k), None, A.add)) for k in range(4)]
+        s["wt"] = G(c, 6, [], lambda g, T: g.iota(T.wt[:, 0:N], [[-1, N]], 8, 0, allow_small_or_imprecise_dtypes=True))
+        s["q512"] = G(c, 6, [], lambda g, T: g.iota(T.q512[:, 0:N], [[K, N]], 0, 0, allow_small_or_imprecise_dtypes=True))
+        s["eq"] = [QZ(c, 128, [s["zt"]], lambda g, T, b=b: g.vector.quantize_mx(T.eq[:, 128 * b:128 * b + 128], T.ep[:, 128 * b:128 * b + 128], T.zt[:, 4 - b:516 - b])) for b in range(4)]
+        for k in range(4):
+            s["ldxs"] = D(c, "Y", [s["qc1"]], lambda g, T, k=k: g.sync.dma_start(T.xsw[:, 128 * k:128 * k + 128], T.x[:, 128 * SWAP[k]:128 * SWAP[k] + 128]), "ld_xs", 64)
+        s["ldc2"] = D(c, "Y", [s["qc1"]], lambda g, T: g.sync.dma_start(T.ct2[:], T.c2[:]), "ld_c2", 16, 1.5)
+        s["qc2"] = QZ(c, 512, [s["ldc2"]], lambda g, T: g.vector.quantize_mx(T.cq2[:], T.cp2[:], T.ct2[:]))
+
+    def make_list(c, i, n, vals, deps, mul, add, fin):
+        sl = i if n == 1 else slice(i, i + n)
+        tr = []
+        for k in range(n):
+            m = X(c, 32, [deps[k], st[c]["mask"]], lambda g, T, k=k: g.vector.tensor_scalar(T.lx[:, i + k, :], T.mask[:], vals[k](T), None, A.mult),
+                  lambda g, T, k=k: g.scalar.activation(T.lx[:, i + k, :], T.mask[:], F.Copy, scale=vals[k](T)))
+            tr.append(V(c, 32, [m], lambda g, T, k=k: g.vector.transpose(T.lt[:, i + k, :], T.lx[:, i + k, :])))
+        y = V(c, 16 * n, tr, lambda g, T: g.vector.tensor_tensor(T.ly[:, sl, :], T.lt[:, sl, 0::2], T.lt[:, sl, 1::2], A.add))
+        half = {}
+        for h in range(2):
+            for d in range(2):
+                half[(h, d)] = V(c, 8 * n, [y], lambda g, T, h=h, d=d: g.vector.tensor_tensor(
+                    T.ls[64 * d:64 * d + 64, sl, 8 * h:8 * h + 8], T.ly[64 * h:64 * h + 64, sl, 0::2], T.ly[64 * h:64 * h + 64, sl, 1::2], A.add))
+        out = []
+        for d in range(2):
+            for b in range(2):
+                for a in range(2):
+                    o, f = 64 * d + 32 * b, 64 * d + 32 * a
+                    out.append(X(c, 16 * n, [half[(0, d)], half[(1, d)], fin],
+                                 lambda g, T, o=o, f=f, a=a: g.vector.tensor_scalar(T.lf[o:o + 32, sl, 16 * a:16 * a + 16], T.ls[f:f + 32, sl, :], mul, add(T)[f:f + 32, 0:1], A.mult, A.add),
+                                 lambda g, T, o=o, f=f, a=a: g.scalar.activation(T.lf[o:o + 32, sl, 16 * a:16 * a + 16], T.ls[f:f + 32, sl, :], F.Identity, bias=add(T)[f:f + 32, 0:1], scale=mul)))
+        return [V(c, 32 * n, out, lambda g, T: g.vector.tensor_copy(T.off[:, sl, :], T.lf[:, sl, :]))]
+
+    scans = [[] for _ in R]
+    slot = [0] * N
+    pairs = {1: [[] for _ in R], 2: [[] for _ in R]}
+
+    def search(c, stage, group):
+        s = st[c]
+        sg = {}
+        for r in group:
+            rm, bank = "rm%d_%d" % (stage, r), len(scans[c]) % 4
+            prev = scans[c][-4] if len(scans[c]) >= 4 else None
+            m = MM(c, 512, [s["x%d_%d" % (stage, r)], s["qc%d" % stage], prev], lambda g, T, r=r, bank=bank: g.tensor.matmul_mx(
+                T.sb[:, 512 * bank:512 * bank + 512], T["xq%d" % stage][:, 128 * r:128 * r + 128], T["xp%d" % stage][:, 128 * r:128 * r + 128], T["cq%d" % stage][:], T["cp%d" % stage][:], True, True))
+            sc = V(c, 512, [m, s["neg"]], lambda g, T, rm=rm, bank=bank: g.vector.tensor_tensor_scan(
+                T[rm][:, 0:512], T.sb[:, 512 * bank:512 * bank + 512], T.neg[:], -1e29, A.max, A.max))
+            scans[c].append(sc)
+            sg[r] = S(c, 512, [sc], lambda g, T, rm=rm, r=r: g.scalar.activation(
+                T["jk%d_%d" % (stage, r)][:], T[rm][:, 0:512], F.Sign, bias=T[rm][:, 511:512], scale=-1.0, accum_out=T[rm][:, 512:513]))
+        away = [r for r in group if r != c]
+        if away:
+            o = send(c, [([r], "pair%d" % stage, lambda T, r=r: T["rm%d_%d" % (stage, r)][:, 511:513], lambda T: T["sc%d" % stage][:, 4 * c:4 * c + 2]) for r in away], [sg[r] for r in away])
+            for r in away:
+                pairs[stage][r].append(o)
+        if c in group:
+            s["own%d" % stage] = V(c, 2, [sg[c]], lambda g, T: g.vector.tensor_copy(T["sc%d" % stage][:, 4 * c:4 * c + 2], T["rm%d_%d" % (stage, c)][:, 511:513]))
+        i = slot[c]
+        slot[c] += len(group)
+        ls = make_list(c, i, len(group), [lambda T, r=r: T["rm%d_%d" % (stage, r)][:, 512:513] for r in group], [sg[r] for r in group], 4.0, lambda T: T.acol, s["acol"])
+        qs = {}
+        for k, r in enumerate(group):
+            ga = [X(c, 256, ls,
+                    lambda g, T, k=k, r=r, e=e: g.vector.tensor_copy(T["gt%d_%d" % (stage, r)][:, 256 * e:256 * e + 256], T["ct%d" % stage][:, 0:4 * K].indirect(T.off[:, i + k, 16 * e:16 * e + 16])),
+                    lambda g, T, k=k, r=r, e=e: g.scalar.activation(T["gt%d_%d" % (stage, r)][:, 256 * e:256 * e + 256], T["ct%d" % stage][:, 0:4 * K].indirect(T.off[:, i + k, 16 * e:16 * e + 16]), F.Copy), True) for e in range(2)]
+            if r == c:
+                qs[r] = QZ(c, 128, ga, lambda g, T: g.vector.quantize_mx(T["wq%d" % stage][:, 128 * c:128 * c + 128], T["wp%d" % stage][:, 128 * c:128 * c + 128], T["gt%d_%d" % (stage, c)][:]))
+                s["w%d_%d" % (stage, c)] = qs[r]
+            else:
+                qs[r] = QZ(c, 128, ga, lambda g, T, r=r: g.vector.quantize_mx(T["oq%d_%d" % (stage, r)][:], T["op%d_%d" % (stage, r)][:], T["gt%d_%d" % (stage, r)][:]))
+        if away:
+            sem = "wa%d_%d" % (stage, c)
+            a, b = 128 * c, 128 * c + 128
+            s1 = send(c, [([r], sem, lambda T, r=r: T["oq%d_%d" % (stage, r)][:].bitcast(dt.uint8), lambda T: T["wq%d" % stage][:, a:b].bitcast(dt.uint8)) for r in away], [qs[r] for r in away])
+            s2 = send(c, [([r], sem, lambda T, r=r: T["op%d_%d" % (stage, r)][:], lambda T: T["wp%d" % stage][:, a:b]) for r in away], [qs[r] for r in away])
+            for r in away:
+                st[r]["w%d_%d" % (stage, c)] = arrive(r, sem, [s1, s2], E["hop"])
+
+    upd = [{} for _ in R]
+
+    def finish(c, stage):
+        s = st[c]
+        dc, sc = "dc%d" % stage, "sc%d" % stage
+        pa = arrive(c, "pair%d" % stage, pairs[stage][c], E["hop"])
+        col = lambda T, k: T[dc][:, k:k + 1]
+        m = V(c, 6, [pa, s["own%d" % stage]], lambda g, T: g.vector.tensor_reduce(col(T, 0), T[sc][:, 0::4], AxisListType.X, A.max))
+        e = V(c, 6, [m], lambda g, T: g.vector.tensor_scalar(T[dc][:, 8:8 + N], T[sc][:, 0::4], col(T, 0), None, A.is_equal))
+        w = V(c, 6, [e, s["wt"]], lambda g, T: g.vector.tensor_tensor(T[dc][:, 16:16 + N], T[dc][:, 8:8 + N], T.wt[:, 0:N], A.mult))
+        k8 = V(c, 6, [w], lambda g, T: g.vector.tensor_reduce(col(T, 1), T[dc][:, 16:16 + N], AxisListType.X, A.max))
+        v = V(c, 1, [k8] + s["nc"], lambda g, T: g.vector.tensor_scalar(col(T, 2), col(T, 1), -128.0, T.nc[:, 1:2], A.mult, A.add))
+        i = slot[c]
+        slot[c] += 1
+        ls = make_list(c, i, 1, [lambda T: col(T, 2)], [v], 1.0, lambda T: T.a768, s["a768"])
+        oh = V(c, 6, [k8], lambda g, T: g.vector.tensor_scalar(T[dc][:, 24:24 + N], T[dc][:, 16:16 + N], col(T, 1), None, A.is_equal))
+        gn = V(c, 6, [pa, s["own%d" % stage], s["q512"]], lambda g, T: g.vector.tensor_tensor(T[dc][:, 32:32 + N], T[sc][:, 1::4], T.q512[:, 0:N], A.add))
+        pr = V(c, 6, [oh, gn], lambda g, T: g.vector.tensor_tensor(T[dc][:, 24:24 + N], T[dc][:, 24:24 + N], T[dc][:, 32:32 + N], A.mult))
+        nu = V(c, 6, [pr], lambda g, T: g.vector.tensor_reduce(col(T, 3), T[dc][:, 24:24 + N], AxisListType.X, A.add))
+        for row, cc, dep in ((stage - 1, 3, nu), (stage + 1, 0, m)):
+            if stage == 1:
+                D(c, "Y", [dep], lambda g, T, row=row, cc=cc: g.sync.dma_start(T.no[row:row + 1, :], col(T, cc)), "st_no", 160)
+            else:
+                for q in range(4):
+                    D(c, "Y", [dep], lambda g, T, row=row, cc=cc, q=q: g.sync.dma_start(T.no[row:row + 1, 32 * SWAP[q]:32 * SWAP[q] + 32], T[dc][32 * q:32 * q + 32, cc:cc + 1]), "st_no", 160)
+        cps = []
+        for h in range(3):
+            for b in range(4):
+                u = MM(c, 256, [s["w%d_%d" % (stage, q)] for q in (2 * h, 2 * h + 1)] + [s["eq"][b], upd[c].get(b)], lambda g, T, b=b, h=h: g.tensor.matmul_mx(
+                    T.up[:, 512 * b:512 * b + 256], T.eq[:, 128 * b:128 * b + 128], T.ep[:, 128 * b:128 * b + 128],
+                    T["wq%d" % stage][:, 256 * h:256 * h + 256], T["wp%d" % stage][:, 256 * h:256 * h + 256], True, True))
+                o = lambda T, b=b, h=h: T["win%d" % stage][:, 768 * b + 256 * h:768 * b + 256 * h + 256]
+                p = lambda T, b=b: T.up[:, 512 * b:512 * b + 256]
+                cp = X(c, 256, [u], lambda g, T, o=o, p=p: g.vector.tensor_scalar(o(T), p(T), -1.0, None, A.mult),
+                       lambda g, T, o=o, p=p: g.scalar.activation(o(T), p(T), F.Copy, scale=-1.0))
+                upd[c][b] = cp
+                cps.append(cp)
+        if stage == 1:
+            r = V(c, 900, cps + ls + [s["ldxs"]], lambda g, T: g.vector.tensor_tensor(T.rt[:], T.win1[:, 0:512 * N].indirect(T.off[:, i, 0:32]), T.xsw[:], A.add))
+            q2 = QZ(c, 128, [r], lambda g, T: g.vector.quantize_mx(T.xq2[:, 128 * c:128 * c + 128], T.xp2[:, 128 * c:128 * c + 128], T.rt[:]))
+            spread(c, 2, q2)
+            for k in range(4):
+                s["ldrs"] = D(c, "Y", [r], lambda g, T, k=k: g.sync.dma_start(T.rsw[:, 128 * k:128 * k + 128], T.rt[:, 128 * SWAP[k]:128 * SWAP[k] + 128]), "ld_rs", 64)
+        else:
+            for k in range(2):
+                y = V(c, 450, cps + ls + [s["ldrs"]], lambda g, T, k=k: g.vector.tensor_tensor(
+                    T.yt[:, 256 * k:256 * k + 256], T.win2[:, 0:512 * N].indirect(T.off[:, i, 16 * k:16 * k + 16]), T.rsw[:, 256 * k:256 * k + 256], A.add))
+                if k == 0:
+                    D(c, "Y", [y], lambda g, T: g.sync.dma_start(T.y[:, 0:256], T.yt[:, 0:256]), "st_y0")
+                else:
+                    D(c, "S", [y], lambda g, T: g.scalar.dma_start(T.y[:, 256:512], T.yt[:, 256:512]), "st_y1")
+
+    for c in R:
+        now[0] = 0
+        search(c, 1, [c])
+        for gr in GROUPS[1]:
+            now[0] += 1
+            gr = [r for r in gr if r != c]
+            if gr:
+                search(c, 1, gr)
+    now[0] = 0
+    for c in R:
+        finish(c, 1)
+    for c in R:
+        now[0] = 0
+        for gr in GROUPS[2]:
+            now[0] += 1
+            search(c, 2, list(gr))
+    now[0] = 0
+    for c in R:
+        finish(c, 2)
+    for o in arr:
+        ops[o]["sem"] = (ops[o]["sem"][0], got[(ops[o]["c"], ops[o]["sem"][0])])
+    return ops, sent
+
+
+def order(ops, E):
+    n = len(ops)
+    succ = [[] for _ in range(n)]
+    left = [0] * n
+    for i, o in enumerate(ops):
+        o["deps"] = sorted(set(o["deps"]))
+        left[i] = len(o["deps"])
+        for d in o["deps"]:
+            succ[d].append(i)
+    lst = [i for i in range(n) if left[i] == 0]
+    cnt = list(left)
+    for i in lst:
+        for j in succ[i]:
+            cnt[j] -= 1
+            if cnt[j] == 0:
+                lst.append(j)
+    rank = [0.0] * n
+    for j in reversed(lst):
+        rank[j] = ops[j]["dur"] + ops[j]["lat"] + E["wake"] + max([rank[k] for k in succ[j]] + [0.0])
+    ready = {}
+    free = {}
+    at = [0.0] * n
+    done = [0.0] * n
+    seq = {}
+    todo = n
+
+    def add(i):
+        for q in ops[i].get("alt", (ops[i]["q"],)):
+            ready.setdefault((ops[i]["c"], q), []).append(i)
+    for i in range(n):
+        if left[i] == 0:
+            add(i)
+    while todo:
+        best = None
+        for key, lst in ready.items():
+            if lst:
+                t = max(free.get(key, 0.0) if key[1] else 0.0, min(at[i] for i in lst))
+                if best is None or t < best[0]:
+                    best = (t, key)
+        t, key = best
+        i = max((j for j in ready[key] if at[j] <= t),
+                key=lambda j: (rank[j] - ops[j]["bias"] - (E["alt"] if key[1] == "V" and "alt" in ops[j] else 0.0), -j))
+        o = ops[i]
+        for q in o.get("alt", (o["q"],)):
+            ready[(o["c"], q)].remove(i)
+        if "alt" in o:
+            o["q"] = key[1]
+            o["dur"], o["emit"] = o["alt"][key[1]]
+        if key[1]:
+            seq.setdefault(key, []).append(i)
+            free[key] = t + o["dur"]
+        done[i] = t + o["dur"] + o["lat"]
+        todo -= 1
+        for k in succ[i]:
+            left[k] -= 1
+            at[k] = max(at[k], done[i] + (0.06 if o["q"] == ops[k]["q"] and "alt" not in ops[k] else E["wake"]))
+            if left[k] == 0:
+                add(k)
+    return seq, max(done), done
+
+
+def plan(topo, cores):
+    if "plan" not in _memo:
+        ops, sent = build(topo, cores, EST)
+        seq, span, done = order(ops, EST)
+        _memo["plan"] = (ops, sent, seq, span)
+    return _memo["plan"]
+
+
+def rank_program(g, core, T, topo):
+    rank = T.rank_of(core)
+    if rank is None:
+        return
+    ops, sent, seq, span = plan(topo, list(T.cores))
+    queues = {"V": g.vector, "S": g.scalar, "P": g.tensor, "G": g, "Y": g.sync}
+    num = {}
+    tot = {"sent": sent[rank]}
+    for q in CSEM:
+        k = 0
+        for i in seq.get((rank, q), []):
+            if ops[i]["kind"] == "c":
+                k += 1
+                num[i] = (CSEM[q], k)
+        tot[CSEM[q]] = k
+    known = {q: {} for q in queues}
+    snap = {}
+    pos = {q: 0 for q in queues}
+    mine = sum(len(seq.get((rank, q), [])) for q in queues)
+    while mine:
+        moved = False
+        for q in queues:
+            lst = seq.get((rank, q), [])
+            while pos[q] < len(lst) and all(ops[d]["kind"] in "ra" or d in snap for d in ops[lst[pos[q]]]["deps"]):
+                i = lst[pos[q]]
+                o = ops[i]
+                need = {}
+                for d in o["deps"]:
+                    name, cnt = num[d] if ops[d]["kind"] == "c" else ops[d]["sem"]
+                    if need.get(name, (0, None))[0] < cnt:
+                        need[name] = (cnt, snap.get(d))
+                for name in sorted(need, key=lambda t: -len(need[t][1] or {})):
+                    cnt, sn = need[name]
+                    if known[q].get(name, 0) < cnt:
+                        queues[q].wait_ge(T.sem[name], cnt)
+                        known[q][name] = cnt
+                        for k2, v2 in (sn or {}).items():
+                            known[q][k2] = max(known[q].get(k2, 0), v2)
+                ins = o["emit"](g, T)
+                if o["kind"] == "c":
+                    ins.then_inc(T.sem[num[i][0]], 1)
+                elif o["kind"] == "d":
+                    ins.then_inc(T.sem[o["sem"][0]], 16)
+                snap[i] = dict(known[q])
+                pos[q] += 1
+                mine -= 1
+                moved = True
+        if not moved:
+            raise ValueError("the plan does not close")
+    for o in ops:
+        if o["c"] == rank and o["kind"] in "da":
+            tot[o["sem"][0]] = o["sem"][1]
+    for name in SEMAPHORES:
+        if tot.get(name, 0) > known["G"].get(name, 0):
+            g.wait_ge(T.sem[name], tot[name])

@@ -5,66 +5,99 @@ N = 6
 K = 512
 A = AluOpType
 F = ActivationFunctionType
+CW = 384
 
 SCRATCH = {
     "xt": ("sbuf", [128, 512], "bfloat16"),
-    "xsw": ("sbuf", [128, 512], "bfloat16"),
-    "rt": ("sbuf", [128, 512], "bfloat16"),
-    "rsw": ("sbuf", [128, 512], "bfloat16"),
-    "yt": ("sbuf", [128, 512], "float32"),
-    "neg": ("sbuf", [128, 512], "float32"),
     "ones": ("sbuf", [128, 516], "bfloat16"),
     "zt": ("sbuf", [128, 516], "bfloat16"),
     "eq": ("sbuf", [128, 512], "float8_e4m3fn_x4"),
     "ep": ("sbuf", [128, 512], "uint8"),
+    "neg": ("sbuf", [128, 512], "float32"),
     "bm": ("sbuf", [128, 32], "float32"),
     "mask": ("sbuf", [128, 32], "float32"),
     "pi": ("sbuf", [128, 8], "int32"),
     "p3": ("sbuf", [128, 8], "int32"),
     "acol": ("sbuf", [128, 8], "float32"),
-    "a768": ("sbuf", [128, 8], "float32"),
-    "nc": ("sbuf", [128, 8], "float32"),
+    "aw": ("sbuf", [128, 8], "float32"),
+    "sl": ("sbuf", [128, 16], "float32"),
     "wt": ("sbuf", [128, 8], "float32"),
     "q512": ("sbuf", [128, 8], "float32"),
-    "lx": ("sbuf", [128, 14, 32], "float32"),
-    "lt": ("sbuf", [128, 14, 32], "float32"),
-    "ly": ("sbuf", [128, 14, 16], "float32"),
-    "ls": ("sbuf", [128, 14, 16], "float32"),
-    "lf": ("sbuf", [128, 14, 32], "float32"),
-    "off": ("sbuf", [128, 14, 32], "uint16"),
+    "lx": ("sbuf", [128, 16, 32], "float32"),
+    "lt": ("sbuf", [128, 16, 32], "float32"),
+    "ly": ("sbuf", [128, 16, 16], "float32"),
+    "lz": ("sbuf", [128, 16, 8], "float32"),
+    "ls": ("sbuf", [128, 16, 16], "float32"),
+    "off": ("sbuf", [128, 16, 32], "uint16"),
     "sb": ("psum", [128, 2048], "float32"),
     "up": ("psum", [128, 2048], "float32"),
 }
+for _h in range(2):
+    SCRATCH["rt%d" % _h] = ("sbuf", [128, 512], "bfloat16")
+    SCRATCH["yt%d" % _h] = ("sbuf", [128, 256], "float32")
 for _s in (1, 2):
     SCRATCH["ct%d" % _s] = ("sbuf", [128, 4 * K], "bfloat16")
     SCRATCH["cq%d" % _s] = ("sbuf", [128, K], "float8_e4m3fn_x4")
     SCRATCH["cp%d" % _s] = ("sbuf", [128, K], "uint8")
-    SCRATCH["xq%d" % _s] = ("sbuf", [128, 128 * N], "float8_e4m3fn_x4")
-    SCRATCH["xp%d" % _s] = ("sbuf", [128, 128 * N], "uint8")
-    SCRATCH["wq%d" % _s] = ("sbuf", [128, 128 * N], "float8_e4m3fn_x4")
-    SCRATCH["wp%d" % _s] = ("sbuf", [128, 128 * N], "uint8")
-    SCRATCH["win%d" % _s] = ("sbuf", [128, 512 * N], "bfloat16")
-    SCRATCH["sc%d" % _s] = ("sbuf", [128, 4 * N], "float32")
-    SCRATCH["dc%d" % _s] = ("sbuf", [128, 40], "float32")
-    for _r in range(N):
-        SCRATCH["rm%d_%d" % (_s, _r)] = ("sbuf", [128, 516], "float32")
-        SCRATCH["jk%d_%d" % (_s, _r)] = ("sbuf", [128, 512], "bfloat16")
-        SCRATCH["gt%d_%d" % (_s, _r)] = ("sbuf", [128, 512], "bfloat16")
-        SCRATCH["oq%d_%d" % (_s, _r)] = ("sbuf", [128, 128], "float8_e4m3fn_x4")
-        SCRATCH["op%d_%d" % (_s, _r)] = ("sbuf", [128, 128], "uint8")
+    SCRATCH["xq%d" % _s] = ("sbuf", [128, 896], "float8_e4m3fn_x4")
+    SCRATCH["xp%d" % _s] = ("sbuf", [128, 896], "uint8")
+    SCRATCH["dc%d" % _s] = ("sbuf", [128, 56], "float32")
+    for _h in range(2):
+        SCRATCH["wq%d_%d" % (_s, _h)] = ("sbuf", [128, 448], "float8_e4m3fn_x4")
+        SCRATCH["wp%d_%d" % (_s, _h)] = ("sbuf", [128, 448], "uint8")
+        SCRATCH["win%d_%d" % (_s, _h)] = ("sbuf", [128, 4 * CW], "bfloat16")
+        SCRATCH["sc%d_%d" % (_s, _h)] = ("sbuf", [128, 4 * N], "float32")
+        for _t in range(3):
+            _n = (_s, _h, _t)
+            SCRATCH["rm%d_%d_%d" % _n] = ("sbuf", [128, 516], "float32")
+            SCRATCH["jk%d_%d_%d" % _n] = ("sbuf", [128, 512], "bfloat16")
+            SCRATCH["gt%d_%d_%d" % _n] = ("sbuf", [128, 512], "bfloat16")
+            if _t < 2:
+                SCRATCH["oq%d_%d_%d" % _n] = ("sbuf", [128, 128], "float8_e4m3fn_x4")
+                SCRATCH["op%d_%d_%d" % _n] = ("sbuf", [128, 128], "uint8")
 
-SEMAPHORES = ["cv", "cs", "cp", "cg", "sent", "ld_x", "ld_xs", "ld_c1", "ld_c2", "ld_rs", "st_no", "st_y0", "st_y1"]
+SEMAPHORES = ["cv", "cs", "cp", "cg", "sent", "ld_x", "ld_c1", "ld_c2", "st_no"]
 for _s in (1, 2):
-    SEMAPHORES += ["pair%d" % _s]
-    for _r in range(N):
-        SEMAPHORES += ["xa%d_%d" % (_s, _r), "wa%d_%d" % (_s, _r)]
+    for _h in range(2):
+        SEMAPHORES += ["pair%d_%d" % (_s, _h), "wa%d_%d" % (_s, _h), "st_y%d_%d" % (_s - 1, _h)]
+for _r in range(N):
+    SEMAPHORES += ["xa1_%d" % _r, "xa2_0_%d" % _r, "xa2_1_%d" % _r]
 
 CSEM = {"V": "cv", "S": "cs", "P": "cp", "G": "cg"}
-GROUPS = {1: [[0, 1], [2, 3], [4, 5]], 2: [[0, 1], [2, 3], [4, 5]]}
-EST = {"v0": 0.0, "v": 0.00104, "s0": 0.03, "s": 0.00104, "sg": 0.0019, "mm": 0.00095, "g0": 0.16, "g": 0.0018,
-       "wake": 0.08, "rem": 0.25, "hop": 2.2, "hopx": 3.0, "dma": 2.0, "dmai": 0.08, "bias": 0.25, "alt": 2.0}
-SWAP = (0, 2, 1, 3)
+
+
+def estimate(f, hop, rem, wake):
+    return {"v": 0.00083 * f, "s0": 0.024 * f, "s": 0.00083 * f, "sg": 0.00126 * f, "mm": 0.00076 * f, "g0": 0.13 * f,
+            "g": 0.0015 * f, "wake": wake, "rem": rem, "hop": 2.2 + hop, "hopx": 3.0 + hop, "hopr": 2.8 + hop, "dma": 2.0,
+            "dmai": 0.08, "bias": 0.25}
+
+
+SETS = [estimate(1.2, 0.0, 0.3, 0.08), estimate(1.0, -0.4, 0.25, 0.06), estimate(1.5, 0.3, 0.3, 0.08), estimate(1.2, 0.8, 0.6, 0.1)]
+STEPS = 15000
+LEAD = 2
 _memo = {}
+
+
+def chain(c):
+    turn = lambda p: sorted([r for r in range(N) if r % 2 == p and r != c], key=lambda r: (r - c) % N)
+    o, s = turn(1 - c % 2), turn(c % 2)
+    return [o[0], s[0], o[1], s[1], o[2]]
+
+
+def left(r, h):
+    return (r % 2 == 0) == (h == 0)
+
+
+def own(r, h):
+    return (64, 1) if left(r, h) else (768, 0)
+
+
+def place(r, h, q):
+    return (q - r - 1) % N if left(r, h) else (q - r) % N
+
+
+def lands(r, h):
+    return (0, 320) if left(r, h) else (128, 0)
 
 
 def build(topo, cores, E):
@@ -81,18 +114,17 @@ def build(topo, cores, E):
         return len(ops) - 1
 
     def V(c, n, deps, emit, fast=False):
-        return op(c, "V", E["v0"] + max(64, n * (0.5 if fast else 1)) * E["v"], deps, emit)
+        return op(c, "V", max(64, n * (0.5 if fast else 1)) * E["v"], deps, emit)
 
     def S(c, n, deps, emit):
         return op(c, "S", E["s0"] + max(64, n) * E["s"], deps, emit)
 
     def X(c, n, deps, ev, es, ind=False):
         i = op(c, "V", 0.0, deps, None)
-        dv, ds = E["v0"] + max(64, n) * E["v"], E["s0"] + max(64, n) * E["s"]
+        dv, ds = max(64, n) * E["v"], E["s0"] + max(64, n) * E["s"]
         if ind:
             dv, ds = 0.05 + n * E["sg"], 0.065 + n * E["sg"]
         ops[i]["alt"] = {"V": (dv, ev), "S": (ds, es)}
-        ops[i]["dur"] = min(dv, ds)
         return i
 
     def G(c, n, deps, emit):
@@ -105,7 +137,7 @@ def build(topo, cores, E):
         return op(c, q, E["dmai"], deps, emit, "d", (sem, total), E["dma"] + more)
 
     def QZ(c, n, deps, emit):
-        return op(c, "V", 0.015 + 4 * n * 0.00028, deps, emit)
+        return op(c, "V", 0.015 + 4 * n * 0.00034 * E["v"] / 0.001, deps, emit)
 
     def send(c, parts, deps):
         share = 1
@@ -124,7 +156,7 @@ def build(topo, cores, E):
                 for d in dst:
                     rid, pid, _ = topo.addr(cores[d])
                     ids.append(DstId(rid=rid, pnc=pid))
-                ts.append(RemoteDMATransfer(dst_ids=ids, dma_engine_mask=m, remote_sem=T.sem[sem], srcs=[src(T)], dsts=[land(T) for _ in dst], alu_op=0))
+                ts.append(RemoteDMATransfer(dst_ids=ids, dma_engine_mask=m, remote_sem=T.sem[sem], srcs=[src(T)], dsts=[land(T, d) for d in dst], alu_op=0))
             return g.remote_dma_fused(ts, local_sem=T.sem.sent)
         for dst, sem, _, _ in parts:
             w = len(topo.engines(cores[c], cores[dst[0]])) // share
@@ -143,7 +175,7 @@ def build(topo, cores, E):
         s = st[c]
         s["ldx"] = D(c, "Y", [], lambda g, T: g.sync.dma_start(T.xt[:], T.x[:]), "ld_x")
         s["ldc1"] = D(c, "Y", [], lambda g, T: g.sync.dma_start(T.ct1[:], T.c1[:]), "ld_c1", 16, 1.2)
-        s["qx1"] = QZ(c, 128, [s["ldx"]], lambda g, T, c=c: g.vector.quantize_mx(T.xq1[:, 128 * c:128 * c + 128], T.xp1[:, 128 * c:128 * c + 128], T.xt[:]))
+        s["qx1"] = [QZ(c, 128, [s["ldx"]], lambda g, T, a=a: g.vector.quantize_mx(T.xq1[:, a:a + 128], T.xp1[:, a:a + 128], T.xt[:])) for a in (0, 768)]
         s["neg"] = V(c, 512, [], lambda g, T: g.vector.memset(T.neg[:], -1e29))
         s["ones"] = V(c, 516, [], lambda g, T: g.vector.memset(T.ones[:], 1.0), True)
         pi = G(c, 1, [], lambda g, T: g.iota(T.pi[:, 0:1], [[0, 1]], 0, 1))
@@ -151,245 +183,393 @@ def build(topo, cores, E):
         p3 = V(c, 1, [pi], lambda g, T: g.vector.tensor_scalar(T.p3[:, 0:1], T.pi[:, 0:1], 3, None, A.bitwise_and))
         s["acol"] = V(c, 1, [p3], lambda g, T: g.vector.tensor_copy(T.acol[:, 0:1], T.p3[:, 0:1]))
         s["mask"] = V(c, 32, [bm, s["acol"]], lambda g, T: g.vector.tensor_scalar(T.mask[:], T.bm[:], T.acol[:, 0:1], None, A.is_equal))
-        s["a768"] = V(c, 1, [s["acol"]], lambda g, T: g.vector.tensor_scalar(T.a768[:, 0:1], T.acol[:, 0:1], 128.0 * N, None, A.mult))
+        s["aw"] = V(c, 1, [s["acol"]], lambda g, T: g.vector.tensor_scalar(T.aw[:, 0:1], T.acol[:, 0:1], float(CW), None, A.mult))
         s["qc1"] = QZ(c, 512, [s["ldc1"]], lambda g, T: g.vector.quantize_mx(T.cq1[:], T.cp1[:], T.ct1[:]))
 
-    def spread(c, stage, q):
-        dst = [d for d in R if d != c]
-        sem = "xa%d_%d" % (stage, c)
-        a, b = 128 * c, 128 * c + 128
-        vq = lambda T: T["xq%d" % stage][:, a:b].bitcast(dt.uint8)
-        vp = lambda T: T["xp%d" % stage][:, a:b]
-        s1 = send(c, [(dst, sem, vq, vq)], [q])
-        s2 = send(c, [(dst, sem, vp, vp)], [q])
+    def spread(c, stage, h, q):
+        dst = [(c + i) % N for i in range(1, N)]
+        if h is None:
+            sem, a, n, k = "xa1_%d" % c, 0, 128, 0
+        else:
+            sem, n = "xa2_%d_%d" % (h, c), 64
+            a, k = own(c, h)
+        to = lambda d: 128 + 128 * chain(d).index(c) + 64 * k
+        s1 = send(c, [(dst, sem, lambda T: T["xq%d" % stage][:, a:a + n].bitcast(dt.uint8), lambda T, d: T["xq%d" % stage][:, to(d):to(d) + n].bitcast(dt.uint8))], [q])
+        s2 = send(c, [(dst, sem, lambda T: T["xp%d" % stage][:, a:a + n], lambda T, d: T["xp%d" % stage][:, to(d):to(d) + n])], [q])
         for d in dst:
-            st[d]["x%d_%d" % (stage, c)] = arrive(d, sem, [s1, s2], E["hopx"])
-        st[c]["x%d_%d" % (stage, c)] = q
+            o = arrive(d, sem, [s1, s2], E["hopx"] if h is None else E["hopr"])
+            for e in ((0, 1) if h is None else (h,)):
+                st[d]["x%d_%d_%d" % (stage, e, c)] = o
 
     for c in R:
         s = st[c]
-        spread(c, 1, s["qx1"])
+        spread(c, 1, None, s["qx1"][0])
+        for h in range(2):
+            s["x1_%d_%d" % (h, c)] = s["qx1"][0 if left(c, h) else 1]
         s["zt"] = G(c, 516, [s["ones"]], lambda g, T: g.affine_select(T.zt[:], T.ones[:], [[-1, 516]], A.is_equal, 0.0, 4, 4))
-        p0 = G(c, 1, [], lambda g, T: g.iota(T.nc[:, 0:1], [[0, 1]], 1024, 1, allow_small_or_imprecise_dtypes=True))
-        s["nc"] = [V(c, 1, [p0], lambda g, T, k=k: g.vector.tensor_scalar(T.nc[32 * k:32 * k + 32, 1:2], T.nc[32 * k:32 * k + 32, 0:1], 32.0 * (SWAP[k] - k), None, A.add)) for k in range(4)]
-        s["wt"] = G(c, 6, [], lambda g, T: g.iota(T.wt[:, 0:N], [[-1, N]], 8, 0, allow_small_or_imprecise_dtypes=True))
-        s["q512"] = G(c, 6, [], lambda g, T: g.iota(T.q512[:, 0:N], [[K, N]], 0, 0, allow_small_or_imprecise_dtypes=True))
+        late = [s["qx1"][0]]
+        s["wt"] = G(c, 6, late, lambda g, T: g.iota(T.wt[:, 0:N], [[-1, N]], 8, 0, allow_small_or_imprecise_dtypes=True))
+        for h in range(2):
+            m = min(c + 1, N - 1) if left(c, h) else max(c, 1)
+            s["sl%d" % h] = [G(c, z - a, late, lambda g, T, h=h, a=a, z=z, b=64 * place(c, h, a) - (0 if left(c, h) else 64): g.iota(
+                T.sl[:, 8 * h + a:8 * h + z], [[64, z - a]], b, 1, allow_small_or_imprecise_dtypes=True)) for a, z in ((0, m), (m, N))]
+        s["q512"] = G(c, 6, late, lambda g, T: g.iota(T.q512[:, 0:N], [[K, N]], 0, 0, allow_small_or_imprecise_dtypes=True))
         s["eq"] = [QZ(c, 128, [s["zt"]], lambda g, T, b=b: g.vector.quantize_mx(T.eq[:, 128 * b:128 * b + 128], T.ep[:, 128 * b:128 * b + 128], T.zt[:, 4 - b:516 - b])) for b in range(4)]
-        for k in range(4):
-            s["ldxs"] = D(c, "Y", [s["qc1"]], lambda g, T, k=k: g.sync.dma_start(T.xsw[:, 128 * k:128 * k + 128], T.x[:, 128 * SWAP[k]:128 * SWAP[k] + 128]), "ld_xs", 64)
+        s["z"] = [V(c, 256, [], lambda g, T, h=h, z=(0 if left(c, h) else 256): g.vector.memset(T["rt%d" % h][:, z:z + 256], 0.0), True) for h in range(2)]
         s["ldc2"] = D(c, "Y", [s["qc1"]], lambda g, T: g.sync.dma_start(T.ct2[:], T.c2[:]), "ld_c2", 16, 1.5)
         s["qc2"] = QZ(c, 512, [s["ldc2"]], lambda g, T: g.vector.quantize_mx(T.cq2[:], T.cp2[:], T.ct2[:]))
 
-    def make_list(c, i, n, vals, deps, mul, add, fin):
+    def spread_out(c, i, n, p, vals, deps):
         sl = i if n == 1 else slice(i, i + n)
         tr = []
         for k in range(n):
-            m = X(c, 32, [deps[k], st[c]["mask"]], lambda g, T, k=k: g.vector.tensor_scalar(T.lx[:, i + k, :], T.mask[:], vals[k](T), None, A.mult),
-                  lambda g, T, k=k: g.scalar.activation(T.lx[:, i + k, :], T.mask[:], F.Copy, scale=vals[k](T)))
-            tr.append(V(c, 32, [m], lambda g, T, k=k: g.vector.transpose(T.lt[:, i + k, :], T.lx[:, i + k, :])))
-        y = V(c, 16 * n, tr, lambda g, T: g.vector.tensor_tensor(T.ly[:, sl, :], T.lt[:, sl, 0::2], T.lt[:, sl, 1::2], A.add))
-        half = {}
-        for h in range(2):
-            for d in range(2):
-                half[(h, d)] = V(c, 8 * n, [y], lambda g, T, h=h, d=d: g.vector.tensor_tensor(
-                    T.ls[64 * d:64 * d + 64, sl, 8 * h:8 * h + 8], T.ly[64 * h:64 * h + 64, sl, 0::2], T.ly[64 * h:64 * h + 64, sl, 1::2], A.add))
-        out = []
+            m = X(c, 32, [deps[k], st[c]["mask"]], lambda g, T, k=k: g.vector.tensor_scalar(T.lx[p, i + k, :], T.mask[p, :], vals[k](T), None, A.mult),
+                  lambda g, T, k=k: g.scalar.activation(T.lx[p, i + k, :], T.mask[p, :], F.Copy, scale=vals[k](T)))
+            tr.append(V(c, 32, [m], lambda g, T, k=k: g.vector.transpose(T.lt[p, i + k, :], T.lx[p, i + k, :])))
+        y = V(c, 32 * n, tr, lambda g, T: g.vector.tensor_tensor(T.ly[p, sl, :], T.lt[p, sl, 0::2], T.lt[p, sl, 1::2], A.add))
+        return V(c, 16 * n, [y], lambda g, T: g.vector.tensor_tensor(T.lz[p, sl, :], T.ly[p, sl, 0::2], T.ly[p, sl, 1::2], A.add))
+
+    def word_list(c, i, n, vals, deps):
+        sl = slice(i, i + n)
+        z = spread_out(c, i, n, slice(0, 128), vals, deps)
+        half = []
         for d in range(2):
             for b in range(2):
                 for a in range(2):
-                    o, f = 64 * d + 32 * b, 64 * d + 32 * a
-                    out.append(X(c, 16 * n, [half[(0, d)], half[(1, d)], fin],
-                                 lambda g, T, o=o, f=f, a=a: g.vector.tensor_scalar(T.lf[o:o + 32, sl, 16 * a:16 * a + 16], T.ls[f:f + 32, sl, :], mul, add(T)[f:f + 32, 0:1], A.mult, A.add),
-                                 lambda g, T, o=o, f=f, a=a: g.scalar.activation(T.lf[o:o + 32, sl, 16 * a:16 * a + 16], T.ls[f:f + 32, sl, :], F.Identity, bias=add(T)[f:f + 32, 0:1], scale=mul)))
-        return [V(c, 32 * n, out, lambda g, T: g.vector.tensor_copy(T.off[:, sl, :], T.lf[:, sl, :]))]
+                    o, f = slice(64 * d + 32 * b, 64 * d + 32 * b + 32), slice(64 * d + 32 * a, 64 * d + 32 * a + 32)
+                    half.append(X(c, 8 * n, [z], lambda g, T, o=o, f=f, a=a: g.vector.tensor_copy(T.ls[o, sl, 8 * a:8 * a + 8], T.lz[f, sl, :]),
+                                  lambda g, T, o=o, f=f, a=a: g.scalar.activation(T.ls[o, sl, 8 * a:8 * a + 8], T.lz[f, sl, :], F.Copy)))
+        out = []
+        for h in range(2):
+            for d in range(2):
+                o, f = slice(64 * d, 64 * d + 64), slice(64 * h, 64 * h + 64)
+                out.append(V(c, 16 * n, half[4 * h:4 * h + 4] + [st[c]["acol"]], lambda g, T, o=o, f=f, h=h: g.vector.tensor_scalar(
+                    T.off[o, sl, 16 * h:16 * h + 16], T.ls[f, sl, :], 4.0, T.acol[f, 0:1], A.mult, A.add)))
+        return out
 
     scans = [[] for _ in R]
     slot = [0] * N
-    pairs = {1: [[] for _ in R], 2: [[] for _ in R]}
+    pairs = {(s, h): [[] for _ in R] for s in (1, 2) for h in range(2)}
+    cands = {(s, h): [[] for _ in R] for s in (1, 2) for h in range(2)}
 
-    def search(c, stage, group):
+    def search(c, stage, h):
         s = st[c]
+        ch = chain(c)
+        ot = lands(c, h)[1]
+        tiles = [(192, (ch[0], ch[1])), (448, (ch[2], ch[3])), (704, (ch[4], c))]
+        if left(c, h):
+            tiles = [(320, (ch[1], ch[2])), (576, (ch[3], ch[4])), (64, (c, ch[0]))]
+        seq = [2, 0, 1]
+        nm = lambda k: "%d_%d_%d" % (stage, h, k)
+        wq, wp, sc_ = "wq%d_%d" % (stage, h), "wp%d_%d" % (stage, h), "sc%d_%d" % (stage, h)
         sg = {}
-        for r in group:
-            rm, bank = "rm%d_%d" % (stage, r), len(scans[c]) % 4
+        for k in seq:
+            col, who = tiles[k]
+            bank = len(scans[c]) % 4
             prev = scans[c][-4] if len(scans[c]) >= 4 else None
-            m = MM(c, 512, [s["x%d_%d" % (stage, r)], s["qc%d" % stage], prev], lambda g, T, r=r, bank=bank: g.tensor.matmul_mx(
-                T.sb[:, 512 * bank:512 * bank + 512], T["xq%d" % stage][:, 128 * r:128 * r + 128], T["xp%d" % stage][:, 128 * r:128 * r + 128], T["cq%d" % stage][:], T["cp%d" % stage][:], True, True))
-            sc = V(c, 512, [m, s["neg"]], lambda g, T, rm=rm, bank=bank: g.vector.tensor_tensor_scan(
-                T[rm][:, 0:512], T.sb[:, 512 * bank:512 * bank + 512], T.neg[:], -1e29, A.max, A.max))
+            m = MM(c, 512, [s["x%d_%d_%d" % (stage, h, r)] for r in who] + [s["qc%d" % stage], prev], lambda g, T, col=col, bank=bank: g.tensor.matmul_mx(
+                T.sb[:, 512 * bank:512 * bank + 512], T["xq%d" % stage][:, col:col + 128], T["xp%d" % stage][:, col:col + 128], T["cq%d" % stage][:], T["cp%d" % stage][:], True, True))
+            sc = V(c, 512, [m, s["neg"]], lambda g, T, k=k, bank=bank: g.vector.tensor_tensor_scan(
+                T["rm" + nm(k)][:, 0:512], T.sb[:, 512 * bank:512 * bank + 512], T.neg[:], -1e29, A.max, A.max))
             scans[c].append(sc)
-            sg[r] = S(c, 512, [sc], lambda g, T, rm=rm, r=r: g.scalar.activation(
-                T["jk%d_%d" % (stage, r)][:], T[rm][:, 0:512], F.Sign, bias=T[rm][:, 511:512], scale=-1.0, accum_out=T[rm][:, 512:513]))
-        away = [r for r in group if r != c]
-        if away:
-            o = send(c, [([r], "pair%d" % stage, lambda T, r=r: T["rm%d_%d" % (stage, r)][:, 511:513], lambda T: T["sc%d" % stage][:, 4 * c:4 * c + 2]) for r in away], [sg[r] for r in away])
-            for r in away:
-                pairs[stage][r].append(o)
-        if c in group:
-            s["own%d" % stage] = V(c, 2, [sg[c]], lambda g, T: g.vector.tensor_copy(T["sc%d" % stage][:, 4 * c:4 * c + 2], T["rm%d_%d" % (stage, c)][:, 511:513]))
-        i = slot[c]
-        slot[c] += len(group)
-        ls = make_list(c, i, len(group), [lambda T, r=r: T["rm%d_%d" % (stage, r)][:, 512:513] for r in group], [sg[r] for r in group], 4.0, lambda T: T.acol, s["acol"])
+            sg[k] = S(c, 512, [sc], lambda g, T, k=k: g.scalar.activation(
+                T["jk" + nm(k)][:], T["rm" + nm(k)][:, 0:512], F.Sign, bias=T["rm" + nm(k)][:, 511:512], scale=-1.0, accum_out=T["rm" + nm(k)][:, 512:513]))
+        o = send(c, [([r for r in tiles[k][1] if r != c], "pair%d_%d" % (stage, h), lambda T, k=k: T["rm" + nm(k)][:, 511:513],
+                      lambda T, d: T[sc_][:, 4 * c:4 * c + 2]) for k in range(3)], [sg[k] for k in range(3)])
+        for r in R:
+            if r != c:
+                pairs[(stage, h)][r].append(o)
+        pb = slice(0, 64) if left(c, h) else slice(64, 128)
+        s["own%d_%d" % (stage, h)] = V(c, 2, [sg[2]], lambda g, T: g.vector.tensor_copy(T[sc_][pb, 4 * c:4 * c + 2], T["rm" + nm(2)][pb, 511:513]))
+        i0 = slot[c]
+        slot[c] += 3
+        ls = word_list(c, i0, 3, [lambda T, k=k: T["rm" + nm(k)][:, 512:513] for k in seq], [sg[k] for k in seq])
         qs = {}
-        for k, r in enumerate(group):
+        for j, k in enumerate(seq):
+            i = i0 + j
             ga = [X(c, 256, ls,
-                    lambda g, T, k=k, r=r, e=e: g.vector.tensor_copy(T["gt%d_%d" % (stage, r)][:, 256 * e:256 * e + 256], T["ct%d" % stage][:, 0:4 * K].indirect(T.off[:, i + k, 16 * e:16 * e + 16])),
-                    lambda g, T, k=k, r=r, e=e: g.scalar.activation(T["gt%d_%d" % (stage, r)][:, 256 * e:256 * e + 256], T["ct%d" % stage][:, 0:4 * K].indirect(T.off[:, i + k, 16 * e:16 * e + 16]), F.Copy), True) for e in range(2)]
-            if r == c:
-                qs[r] = QZ(c, 128, ga, lambda g, T: g.vector.quantize_mx(T["wq%d" % stage][:, 128 * c:128 * c + 128], T["wp%d" % stage][:, 128 * c:128 * c + 128], T["gt%d_%d" % (stage, c)][:]))
-                s["w%d_%d" % (stage, c)] = qs[r]
+                    lambda g, T, k=k, i=i, e=e: g.vector.tensor_copy(T["gt" + nm(k)][:, 256 * e:256 * e + 256], T["ct%d" % stage][:, 0:4 * K].indirect(T.off[:, i, 16 * e:16 * e + 16])),
+                    lambda g, T, k=k, i=i, e=e: g.scalar.activation(T["gt" + nm(k)][:, 256 * e:256 * e + 256], T["ct%d" % stage][:, 0:4 * K].indirect(T.off[:, i, 16 * e:16 * e + 16]), F.Copy), True) for e in range(2)]
+            if k == 2:
+                qs[k] = QZ(c, 128, ga, lambda g, T: g.vector.quantize_mx(T[wq][:, ot:ot + 128], T[wp][:, ot:ot + 128], T["gt" + nm(2)][:]))
+                s["w%d_%d" % (stage, h)] = qs[k]
             else:
-                qs[r] = QZ(c, 128, ga, lambda g, T, r=r: g.vector.quantize_mx(T["oq%d_%d" % (stage, r)][:], T["op%d_%d" % (stage, r)][:], T["gt%d_%d" % (stage, r)][:]))
-        if away:
-            sem = "wa%d_%d" % (stage, c)
-            a, b = 128 * c, 128 * c + 128
-            s1 = send(c, [([r], sem, lambda T, r=r: T["oq%d_%d" % (stage, r)][:].bitcast(dt.uint8), lambda T: T["wq%d" % stage][:, a:b].bitcast(dt.uint8)) for r in away], [qs[r] for r in away])
-            s2 = send(c, [([r], sem, lambda T, r=r: T["op%d_%d" % (stage, r)][:], lambda T: T["wp%d" % stage][:, a:b]) for r in away], [qs[r] for r in away])
-            for r in away:
-                st[r]["w%d_%d" % (stage, c)] = arrive(r, sem, [s1, s2], E["hop"])
+                qs[k] = QZ(c, 128, ga, lambda g, T, k=k: g.vector.quantize_mx(T["oq" + nm(k)][:], T["op" + nm(k)][:], T["gt" + nm(k)][:]))
+        sem = "wa%d_%d" % (stage, h)
+        to = lambda d: lands(d, h)[0] + 64 * ((c - d - 1) % N)
+        for part in ([2], [0, 1]):
+            pc, pp = [], []
+            for k in part:
+                for e, r in enumerate(tiles[k][1]):
+                    if r != c:
+                        a, bq, bp = (ot + 64 * e, wq, wp) if k == 2 else (64 * e, "oq" + nm(k), "op" + nm(k))
+                        pc.append(([r], sem, lambda T, bq=bq, a=a: T[bq][:, a:a + 64].bitcast(dt.uint8), lambda T, d: T[wq][:, to(d):to(d) + 64].bitcast(dt.uint8)))
+                        pp.append(([r], sem, lambda T, bp=bp, a=a: T[bp][:, a:a + 64], lambda T, d: T[wp][:, to(d):to(d) + 64]))
+            s1 = send(c, pc, [qs[k] for k in part])
+            s2 = send(c, pp, [qs[k] for k in part])
+            for p in pc:
+                cands[(stage, h)][p[0][0]] += [s1, s2]
 
     upd = [{} for _ in R]
+    joint = [{} for _ in R]
 
-    def finish(c, stage):
+    def finish(c, stage, h):
         s = st[c]
-        dc, sc = "dc%d" % stage, "sc%d" % stage
-        pa = arrive(c, "pair%d" % stage, pairs[stage][c], E["hop"])
-        col = lambda T, k: T[dc][:, k:k + 1]
-        m = V(c, 6, [pa, s["own%d" % stage]], lambda g, T: g.vector.tensor_reduce(col(T, 0), T[sc][:, 0::4], AxisListType.X, A.max))
-        e = V(c, 6, [m], lambda g, T: g.vector.tensor_scalar(T[dc][:, 8:8 + N], T[sc][:, 0::4], col(T, 0), None, A.is_equal))
-        w = V(c, 6, [e, s["wt"]], lambda g, T: g.vector.tensor_tensor(T[dc][:, 16:16 + N], T[dc][:, 8:8 + N], T.wt[:, 0:N], A.mult))
-        k8 = V(c, 6, [w], lambda g, T: g.vector.tensor_reduce(col(T, 1), T[dc][:, 16:16 + N], AxisListType.X, A.max))
-        v = V(c, 1, [k8] + s["nc"], lambda g, T: g.vector.tensor_scalar(col(T, 2), col(T, 1), -128.0, T.nc[:, 1:2], A.mult, A.add))
+        dc, sc, win = "dc%d" % stage, "sc%d_%d" % (stage, h), "win%d_%d" % (stage, h)
+        pb = slice(0, 64) if left(c, h) else slice(64, 128)
+        p0 = 0 if left(c, h) else 64
+        p1 = 64 - p0
+        pa = arrive(c, "pair%d_%d" % (stage, h), pairs[(stage, h)][c], E["hop"])
+        wa = arrive(c, "wa%d_%d" % (stage, h), cands[(stage, h)][c], E["hop"])
+        col = lambda T, k: T[dc][pb, k:k + 1]
+        ow = s["own%d_%d" % (stage, h)]
+        m = V(c, 6, [pa, ow], lambda g, T: g.vector.tensor_reduce(col(T, 0), T[sc][pb, 0::4], AxisListType.X, A.max))
+        e = V(c, 6, [m], lambda g, T: g.vector.tensor_scalar(T[dc][pb, 8:8 + N], T[sc][pb, 0::4], col(T, 0), None, A.is_equal))
+        w = V(c, 6, [e, s["wt"]], lambda g, T: g.vector.tensor_tensor(T[dc][pb, 16:16 + N], T[dc][pb, 8:8 + N], T.wt[pb, 0:N], A.mult))
+        k8 = V(c, 6, [w], lambda g, T: g.vector.tensor_reduce(col(T, 1), T[dc][pb, 16:16 + N], AxisListType.X, A.max))
+        oh = V(c, 6, [k8], lambda g, T: g.vector.tensor_scalar(T[dc][pb, 24:24 + N], T[dc][pb, 16:16 + N], col(T, 1), None, A.is_equal))
+        pv = V(c, 6, [oh] + s["sl%d" % h], lambda g, T: g.vector.tensor_tensor(T[dc][pb, 40:40 + N], T[dc][pb, 24:24 + N], T.sl[pb, 8 * h:8 * h + N], A.mult))
+        v = V(c, 6, [pv], lambda g, T: g.vector.tensor_reduce(col(T, 2), T[dc][pb, 40:40 + N], AxisListType.X, A.add))
         i = slot[c]
         slot[c] += 1
-        ls = make_list(c, i, 1, [lambda T: col(T, 2)], [v], 1.0, lambda T: T.a768, s["a768"])
-        oh = V(c, 6, [k8], lambda g, T: g.vector.tensor_scalar(T[dc][:, 24:24 + N], T[dc][:, 16:16 + N], col(T, 1), None, A.is_equal))
-        gn = V(c, 6, [pa, s["own%d" % stage], s["q512"]], lambda g, T: g.vector.tensor_tensor(T[dc][:, 32:32 + N], T[sc][:, 1::4], T.q512[:, 0:N], A.add))
-        pr = V(c, 6, [oh, gn], lambda g, T: g.vector.tensor_tensor(T[dc][:, 24:24 + N], T[dc][:, 24:24 + N], T[dc][:, 32:32 + N], A.mult))
-        nu = V(c, 6, [pr], lambda g, T: g.vector.tensor_reduce(col(T, 3), T[dc][:, 24:24 + N], AxisListType.X, A.add))
-        for row, cc, dep in ((stage - 1, 3, nu), (stage + 1, 0, m)):
-            if stage == 1:
-                D(c, "Y", [dep], lambda g, T, row=row, cc=cc: g.sync.dma_start(T.no[row:row + 1, :], col(T, cc)), "st_no", 160)
-            else:
-                for q in range(4):
-                    D(c, "Y", [dep], lambda g, T, row=row, cc=cc, q=q: g.sync.dma_start(T.no[row:row + 1, 32 * SWAP[q]:32 * SWAP[q] + 32], T[dc][32 * q:32 * q + 32, cc:cc + 1]), "st_no", 160)
+        z = spread_out(c, i, 1, pb, [lambda T: col(T, 2)], [v])
+        near = []
+        for b in range(2):
+            for a in range(2):
+                o, f = slice(p0 + 32 * b, p0 + 32 * b + 32), slice(p0 + 32 * a, p0 + 32 * a + 32)
+                near.append(V(c, 8, [z, s["aw"]], lambda g, T, o=o, f=f, a=a: g.vector.tensor_scalar(T.off[o, i, 8 * a:8 * a + 8], T.lz[f, i, :], 1.0, T.aw[f, 0:1], A.mult, A.add)))
+        ls = [V(c, 16, near, lambda g, T: g.vector.tensor_copy(T.off[p1:p1 + 64, i, 0:16], T.off[pb, i, 0:16]))]
+        gn = V(c, 6, [pa, ow, s["q512"]], lambda g, T: g.vector.tensor_tensor(T[dc][pb, 32:32 + N], T[sc][pb, 1::4], T.q512[pb, 0:N], A.add))
+        joint[c].setdefault(stage, []).extend([m, oh, gn])
+        of, ot = lands(c, h)
         cps = []
-        for h in range(3):
+        for mine in (True, False):
             for b in range(4):
-                u = MM(c, 256, [s["w%d_%d" % (stage, q)] for q in (2 * h, 2 * h + 1)] + [s["eq"][b], upd[c].get(b)], lambda g, T, b=b, h=h: g.tensor.matmul_mx(
-                    T.up[:, 512 * b:512 * b + 256], T.eq[:, 128 * b:128 * b + 128], T.ep[:, 128 * b:128 * b + 128],
-                    T["wq%d" % stage][:, 256 * h:256 * h + 256], T["wp%d" % stage][:, 256 * h:256 * h + 256], True, True))
-                o = lambda T, b=b, h=h: T["win%d" % stage][:, 768 * b + 256 * h:768 * b + 256 * h + 256]
-                p = lambda T, b=b: T.up[:, 512 * b:512 * b + 256]
-                cp = X(c, 256, [u], lambda g, T, o=o, p=p: g.vector.tensor_scalar(o(T), p(T), -1.0, None, A.mult),
-                       lambda g, T, o=o, p=p: g.scalar.activation(o(T), p(T), F.Copy, scale=-1.0))
+                a, n = (ot, 128) if mine else (of, 320)
+                f, k, o = (p0, 64, 64 * place(c, h, c)) if mine else (0, 320, 64 * place(c, h, (c + 1) % N))
+                u = MM(c, n, [s["w%d_%d" % (stage, h)] if mine else wa, s["eq"][b], upd[c].get(b)], lambda g, T, b=b, a=a, n=n: g.tensor.matmul_mx(
+                    T.up[:, 512 * b:512 * b + n], T.eq[:, 128 * b:128 * b + 128], T.ep[:, 128 * b:128 * b + 128],
+                    T["wq%d_%d" % (stage, h)][:, a:a + n], T["wp%d_%d" % (stage, h)][:, a:a + n], True, True))
+                to = lambda T, b=b, o=o, k=k: T[win][:, CW * b + o:CW * b + o + k]
+                fr = lambda T, b=b, f=f, k=k: T.up[:, 512 * b + f:512 * b + f + k]
+                cp = X(c, k, [u], lambda g, T, to=to, fr=fr: g.vector.tensor_scalar(to(T), fr(T), -1.0, None, A.mult),
+                       lambda g, T, to=to, fr=fr: g.scalar.activation(to(T), fr(T), F.Copy, scale=-1.0))
                 upd[c][b] = cp
                 cps.append(cp)
+        half = 1 if left(c, h) else 0
         if stage == 1:
-            r = V(c, 900, cps + ls + [s["ldxs"]], lambda g, T: g.vector.tensor_tensor(T.rt[:], T.win1[:, 0:512 * N].indirect(T.off[:, i, 0:32]), T.xsw[:], A.add))
-            q2 = QZ(c, 128, [r], lambda g, T: g.vector.quantize_mx(T.xq2[:, 128 * c:128 * c + 128], T.xp2[:, 128 * c:128 * c + 128], T.rt[:]))
-            spread(c, 2, q2)
-            for k in range(4):
-                s["ldrs"] = D(c, "Y", [r], lambda g, T, k=k: g.sync.dma_start(T.rsw[:, 128 * k:128 * k + 128], T.rt[:, 128 * SWAP[k]:128 * SWAP[k] + 128]), "ld_rs", 64)
+            r = V(c, 450, cps + ls + s["z"] + [s["ldx"]], lambda g, T: g.vector.tensor_tensor(
+                T["rt%d" % h][:, 256 * half:256 * half + 256], T[win][:, 0:4 * CW].indirect(T.off[:, i, 0:16]), T.xt[:, 256 * half:256 * half + 256], A.add))
+            s["r%d" % h] = r
+            a = 0 if left(c, h) else 768
+            q2 = QZ(c, 128, [r], lambda g, T: g.vector.quantize_mx(T.xq2[:, a:a + 128], T.xp2[:, a:a + 128], T["rt%d" % h][:]))
+            s["x2_%d_%d" % (h, c)] = q2
+            spread(c, 2, h, q2)
         else:
             for k in range(2):
-                y = V(c, 450, cps + ls + [s["ldrs"]], lambda g, T, k=k: g.vector.tensor_tensor(
-                    T.yt[:, 256 * k:256 * k + 256], T.win2[:, 0:512 * N].indirect(T.off[:, i, 16 * k:16 * k + 16]), T.rsw[:, 256 * k:256 * k + 256], A.add))
+                y = V(c, 225, cps + ls + [s["r%d" % h]], lambda g, T, k=k: g.vector.tensor_tensor(
+                    T["yt%d" % h][:, 128 * k:128 * k + 128], T[win][:, 0:4 * CW].indirect(T.off[:, i, 8 * k:8 * k + 8]), T["rt%d" % h][:, 256 * half + 128 * k:256 * half + 128 * k + 128], A.add))
+                a = 256 * half + 128 * k
                 if k == 0:
-                    D(c, "Y", [y], lambda g, T: g.sync.dma_start(T.y[:, 0:256], T.yt[:, 0:256]), "st_y0")
+                    D(c, "Y", [y], lambda g, T, a=a, k=k: g.sync.dma_start(T.y[:, a:a + 128], T["yt%d" % h][:, 128 * k:128 * k + 128]), "st_y%d_%d" % (k, h))
                 else:
-                    D(c, "S", [y], lambda g, T: g.scalar.dma_start(T.y[:, 256:512], T.yt[:, 256:512]), "st_y1")
+                    D(c, "S", [y], lambda g, T, a=a, k=k: g.scalar.dma_start(T.y[:, a:a + 128], T["yt%d" % h][:, 128 * k:128 * k + 128]), "st_y%d_%d" % (k, h))
 
-    for c in R:
-        now[0] = 0
-        search(c, 1, [c])
-        for gr in GROUPS[1]:
-            now[0] += 1
-            gr = [r for r in gr if r != c]
-            if gr:
-                search(c, 1, gr)
-    now[0] = 0
-    for c in R:
-        finish(c, 1)
-    for c in R:
-        now[0] = 0
-        for gr in GROUPS[2]:
-            now[0] += 1
-            search(c, 2, list(gr))
-    now[0] = 0
-    for c in R:
-        finish(c, 2)
+    def numbers(c, stage):
+        dc = "dc%d" % stage
+        d = joint[c][stage]
+        pr = V(c, 6, d, lambda g, T: g.vector.tensor_tensor(T[dc][:, 48:48 + N], T[dc][:, 24:24 + N], T[dc][:, 32:32 + N], A.mult))
+        nu = V(c, 6, [pr], lambda g, T: g.vector.tensor_reduce(T[dc][:, 3:4], T[dc][:, 48:48 + N], AxisListType.X, A.add))
+        for row, cc in ((stage - 1, 3), (stage + 1, 0)):
+            for h in range(2):
+                f, o = (0, 64) if left(c, h) else (64, 0)
+                D(c, "Y", [nu] if cc == 3 else d, lambda g, T, row=row, cc=cc, f=f, o=o: g.sync.dma_start(T.no[row:row + 1, o:o + 64], T[dc][f:f + 64, cc:cc + 1]), "st_no", 128)
+
+    for stage in (1, 2):
+        for h in range(2):
+            now[0] = h if stage == 1 else 1 + h
+            for c in R:
+                search(c, stage, h)
+            for c in R:
+                finish(c, stage, h)
+        for c in R:
+            numbers(c, stage)
     for o in arr:
         ops[o]["sem"] = (ops[o]["sem"][0], got[(ops[o]["c"], ops[o]["sem"][0])])
     return ops, sent
 
 
-def order(ops, E):
-    n = len(ops)
-    succ = [[] for _ in range(n)]
-    left = [0] * n
-    for i, o in enumerate(ops):
-        o["deps"] = sorted(set(o["deps"]))
-        left[i] = len(o["deps"])
-        for d in o["deps"]:
+def alike(ops):
+    per = [[i for i, o in enumerate(ops) if o["c"] == c and o["kind"] != "a"] for c in range(N)]
+    calls = [[i for i in l if ops[i]["kind"] == "r"] for l in per]
+    back = {}
+    for l in calls:
+        for k, i in enumerate(l):
+            back[i] = calls[LEAD][k]
+    ids = per[LEAD] + [i for i, o in enumerate(ops) if o["c"] == LEAD and o["kind"] == "a"]
+    at = {i: k for k, i in enumerate(ids)}
+    return per, ids, [sorted(set(at[back.get(d, d)] for d in ops[i]["deps"])) for i in ids]
+
+
+def draw_up(topo, cores):
+    ops, sent = build(topo, cores, SETS[0])
+    per, ids, deps = alike(ops)
+    n = len(ids)
+    R = range(n)
+    sets = []
+    for E in SETS:
+        full = build(topo, cores, E)[0]
+        lead = [full[i] for i in ids]
+        sets.append(([{q: v[0] for q, v in o["alt"].items()} if "alt" in o else {o["q"]: o["dur"]} for o in lead], [o["lat"] for o in lead], E["wake"]))
+    lead = [ops[i] for i in ids]
+    alt = ["alt" in o for o in lead]
+    home = [o["q"] for o in lead]
+    succ = [[] for _ in R]
+    for i in R:
+        for d in deps[i]:
             succ[d].append(i)
-    lst = [i for i in range(n) if left[i] == 0]
-    cnt = list(left)
-    for i in lst:
+    cnt = [len(d) for d in deps]
+    top = [i for i in R if cnt[i] == 0]
+    for i in top:
         for j in succ[i]:
             cnt[j] -= 1
             if cnt[j] == 0:
-                lst.append(j)
+                top.append(j)
     rank = [0.0] * n
-    for j in reversed(lst):
-        rank[j] = ops[j]["dur"] + ops[j]["lat"] + E["wake"] + max([rank[k] for k in succ[j]] + [0.0])
-    ready = {}
-    free = {}
-    at = [0.0] * n
-    done = [0.0] * n
-    seq = {}
-    todo = n
+    for j in reversed(top):
+        rank[j] = min(sets[0][0][j].values()) + sets[0][1][j] + sets[0][2] + max([rank[k] for k in succ[j]] + [0.0])
+    rank = [rank[i] - lead[i]["bias"] for i in R]
 
-    def add(i):
-        for q in ops[i].get("alt", (ops[i]["q"],)):
-            ready.setdefault((ops[i]["c"], q), []).append(i)
-    for i in range(n):
-        if left[i] == 0:
-            add(i)
-    while todo:
-        best = None
-        for key, lst in ready.items():
-            if lst:
-                t = max(free.get(key, 0.0) if key[1] else 0.0, min(at[i] for i in lst))
-                if best is None or t < best[0]:
-                    best = (t, key)
-        t, key = best
-        i = max((j for j in ready[key] if at[j] <= t),
-                key=lambda j: (rank[j] - ops[j]["bias"] - (E["alt"] if key[1] == "V" and "alt" in ops[j] else 0.0), -j))
-        o = ops[i]
-        for q in o.get("alt", (o["q"],)):
-            ready[(o["c"], q)].remove(i)
-        if "alt" in o:
-            o["q"] = key[1]
-            o["dur"], o["emit"] = o["alt"][key[1]]
-        if key[1]:
-            seq.setdefault(key, []).append(i)
-            free[key] = t + o["dur"]
-        done[i] = t + o["dur"] + o["lat"]
-        todo -= 1
-        for k in succ[i]:
-            left[k] -= 1
-            at[k] = max(at[k], done[i] + (0.06 if o["q"] == ops[k]["q"] and "alt" not in ops[k] else E["wake"]))
-            if left[k] == 0:
-                add(k)
-    return seq, max(done), done
+    def order(nudge, pin, favour):
+        dur, lat, wake = sets[0]
+        todo = [len(d) for d in deps]
+        at = [0.0] * n
+        ready = {q: [] for q in ("V", "S", "P", "G", "Y", None)}
+        free = {q: 0.0 for q in ready}
+        seq = {q: [] for q in ready}
+        qof = [None] * n
+        pr = [rank[i] + nudge[i] for i in R]
+
+        def add(i):
+            if not alt[i]:
+                ready[home[i]].append(i)
+                return
+            for q in ("V", "S"):
+                if pin[i] in (None, q):
+                    ready[q].append(i)
+        for i in R:
+            if todo[i] == 0:
+                add(i)
+        for _ in R:
+            bt, bq = 1e9, None
+            for q, l in ready.items():
+                if l:
+                    t = min([at[i] for i in l])
+                    if q and free[q] > t:
+                        t = free[q]
+                    if t < bt:
+                        bt, bq = t, q
+            i, bp = -1, -1e9
+            for j in ready[bq]:
+                if at[j] <= bt:
+                    p = pr[j] - (favour if bq == "V" and alt[j] else 0.0)
+                    if p > bp:
+                        i, bp = j, p
+            ready[bq].remove(i)
+            if alt[i]:
+                o = "S" if bq == "V" else "V"
+                if i in ready[o]:
+                    ready[o].remove(i)
+            qof[i] = bq
+            e = bt + dur[i][bq]
+            if bq:
+                free[bq] = e
+            seq[bq].append(i)
+            for k in succ[i]:
+                todo[k] -= 1
+                at[k] = max(at[k], e + lat[i] + (0.06 if bq == home[k] and not alt[k] else wake))
+                if todo[k] == 0:
+                    add(k)
+        return seq, qof
+
+    def span(seq, qof, which):
+        dur, lat, wake = sets[which]
+        todo = [len(d) for d in deps]
+        at = [0.0] * n
+        pos = {q: 0 for q in seq}
+        free = {q: 0.0 for q in seq}
+        end = 0.0
+        land = [i for i in R if qof[i] is None and todo[i] == 0]
+        moved = True
+        while moved:
+            moved = False
+            for q, l in seq.items():
+                while (land if q is None else pos[q] < len(l) and todo[l[pos[q]]] == 0):
+                    i = land.pop() if q is None else l[pos[q]]
+                    pos[q] += 1
+                    e = at[i] if q is None else max(at[i], free[q]) + dur[i][q]
+                    free[q] = e
+                    moved = True
+                    d = e + lat[i]
+                    if d > end:
+                        end = d
+                    for k in succ[i]:
+                        todo[k] -= 1
+                        a = d + (0.06 if q and qof[k] == q else wake)
+                        if a > at[k]:
+                            at[k] = a
+                        if todo[k] == 0 and qof[k] is None:
+                            land.append(k)
+        return end
+
+    seed = [12345]
+
+    def draw(m):
+        seed[0] = (seed[0] * 1103515245 + 12345) % (1 << 31)
+        return (seed[0] >> 8) % m
+
+    work = [i for i in R if home[i] in ("V", "S")]
+    both = [i for i in work if alt[i]]
+    cur = ([0.0] * n, [None] * n, 1.0)
+    kept = order(*cur)
+    base = [span(kept[0], kept[1], k) for k in range(len(SETS))]
+    now = best = 1.0
+    for step in range(STEPS):
+        nudge, pin, favour = list(cur[0]), list(cur[1]), cur[2]
+        k = draw(100)
+        if k < 60:
+            for _ in range(1 + draw(3)):
+                nudge[work[draw(len(work))]] = (draw(61) - 30) / 10.0 if draw(10) < 7 else 0.0
+        elif k < 75:
+            a, d = draw(len(work)), (draw(51) - 25) / 10.0
+            for i in work[a:a + 3 + draw(38)]:
+                nudge[i] += d
+        elif k < 97:
+            for _ in range(1 + draw(3)):
+                pin[both[draw(len(both))]] = (None, "V", "S")[draw(3)]
+        else:
+            favour = (0.0, 0.5, 1.0, 1.5, 2.0, 3.0)[draw(6)]
+        so = order(nudge, pin, favour)
+        v = sum(span(so[0], so[1], k) / base[k] for k in range(len(SETS))) / len(SETS)
+        if v <= now + 0.003 * max(0.0, 1.0 - step / (0.9 * STEPS)) * draw(1000) / 1000.0:
+            cur, now = (nudge, pin, favour), v
+            if v < best:
+                best, kept = v, so
+    seq = {}
+    for c in range(N):
+        for q, l in kept[0].items():
+            if q:
+                seq[(c, q)] = [per[c][k] for k in l]
+        for k in both:
+            o = ops[per[c][k]]
+            o["q"] = kept[1][k]
+            o["emit"] = o["alt"][o["q"]][1]
+    return ops, sent, seq, [span(kept[0], kept[1], k) for k in range(len(SETS))]
 
 
 def plan(topo, cores):
     if "plan" not in _memo:
-        ops, sent = build(topo, cores, EST)
-        seq, span, done = order(ops, EST)
-        _memo["plan"] = (ops, sent, seq, span)
+        _memo["plan"] = draw_up(topo, cores)
     return _memo["plan"]
 
 
@@ -397,7 +577,7 @@ def rank_program(g, core, T, topo):
     rank = T.rank_of(core)
     if rank is None:
         return
-    ops, sent, seq, span = plan(topo, list(T.cores))
+    ops, sent, seq, _ = plan(topo, list(T.cores))
     queues = {"V": g.vector, "S": g.scalar, "P": g.tensor, "G": g, "Y": g.sync}
     num = {}
     tot = {"sent": sent[rank]}

from concourse.bass import DstId, RemoteDMATransfer
from concourse.mybir import dt, AluOpType, AxisListType, ActivationFunctionType

N = 6
K = 512
A = AluOpType
F = ActivationFunctionType
CW = 384

SCRATCH = {
    "xt": ("sbuf", [128, 512], "bfloat16"),
    "ones": ("sbuf", [128, 516], "bfloat16"),
    "zt": ("sbuf", [128, 516], "bfloat16"),
    "eq": ("sbuf", [128, 512], "float8_e4m3fn_x4"),
    "ep": ("sbuf", [128, 512], "uint8"),
    "neg": ("sbuf", [128, 512], "float32"),
    "bm": ("sbuf", [128, 32], "float32"),
    "mask": ("sbuf", [128, 32], "float32"),
    "pi": ("sbuf", [128, 8], "int32"),
    "p3": ("sbuf", [128, 8], "int32"),
    "acol": ("sbuf", [128, 8], "float32"),
    "aw": ("sbuf", [128, 8], "float32"),
    "sl": ("sbuf", [128, 16], "float32"),
    "wt": ("sbuf", [128, 8], "float32"),
    "q512": ("sbuf", [128, 8], "float32"),
    "lx": ("sbuf", [128, 16, 32], "float32"),
    "lt": ("sbuf", [128, 16, 32], "float32"),
    "ly": ("sbuf", [128, 16, 16], "float32"),
    "lz": ("sbuf", [128, 16, 8], "float32"),
    "ls": ("sbuf", [128, 16, 16], "float32"),
    "off": ("sbuf", [128, 16, 32], "uint16"),
    "sb": ("psum", [128, 2048], "float32"),
    "up": ("psum", [128, 2048], "float32"),
}
for _h in range(2):
    SCRATCH["rt%d" % _h] = ("sbuf", [128, 512], "bfloat16")
    SCRATCH["yt%d" % _h] = ("sbuf", [128, 256], "float32")
for _s in (1, 2):
    SCRATCH["ct%d" % _s] = ("sbuf", [128, 4 * K], "bfloat16")
    SCRATCH["cq%d" % _s] = ("sbuf", [128, K], "float8_e4m3fn_x4")
    SCRATCH["cp%d" % _s] = ("sbuf", [128, K], "uint8")
    SCRATCH["xq%d" % _s] = ("sbuf", [128, 896], "float8_e4m3fn_x4")
    SCRATCH["xp%d" % _s] = ("sbuf", [128, 896], "uint8")
    SCRATCH["dc%d" % _s] = ("sbuf", [128, 56], "float32")
    for _h in range(2):
        SCRATCH["wq%d_%d" % (_s, _h)] = ("sbuf", [128, 448], "float8_e4m3fn_x4")
        SCRATCH["wp%d_%d" % (_s, _h)] = ("sbuf", [128, 448], "uint8")
        SCRATCH["win%d_%d" % (_s, _h)] = ("sbuf", [128, 4 * CW], "bfloat16")
        SCRATCH["sc%d_%d" % (_s, _h)] = ("sbuf", [128, 4 * N], "float32")
        for _t in range(3):
            _n = (_s, _h, _t)
            SCRATCH["rm%d_%d_%d" % _n] = ("sbuf", [128, 516], "float32")
            SCRATCH["jk%d_%d_%d" % _n] = ("sbuf", [128, 512], "bfloat16")
            SCRATCH["gt%d_%d_%d" % _n] = ("sbuf", [128, 512], "bfloat16")
            if _t < 2:
                SCRATCH["oq%d_%d_%d" % _n] = ("sbuf", [128, 128], "float8_e4m3fn_x4")
                SCRATCH["op%d_%d_%d" % _n] = ("sbuf", [128, 128], "uint8")

SEMAPHORES = ["cv", "cs", "cp", "cg", "sent", "ld_x", "ld_c1", "ld_c2", "st_no"]
for _s in (1, 2):
    for _h in range(2):
        SEMAPHORES += ["pair%d_%d" % (_s, _h), "wa%d_%d" % (_s, _h), "st_y%d_%d" % (_s - 1, _h)]
for _r in range(N):
    SEMAPHORES += ["xa1_%d" % _r, "xa2_0_%d" % _r, "xa2_1_%d" % _r]

CSEM = {"V": "cv", "S": "cs", "P": "cp", "G": "cg"}


def estimate(f, hop, rem, wake):
    return {"v": 0.00083 * f, "s0": 0.024 * f, "s": 0.00083 * f, "sg": 0.00126 * f, "mm": 0.00076 * f, "g0": 0.13 * f,
            "g": 0.0015 * f, "wake": wake, "rem": rem, "hop": 2.2 + hop, "hopx": 3.0 + hop, "hopr": 2.8 + hop, "dma": 2.0,
            "dmai": 0.08, "bias": 0.25}


SETS = [estimate(1.2, 0.0, 0.3, 0.08), estimate(1.0, -0.4, 0.25, 0.06), estimate(1.5, 0.3, 0.3, 0.08), estimate(1.2, 0.8, 0.6, 0.1)]
STEPS = 15000
LEAD = 2
_memo = {}


def chain(c):
    turn = lambda p: sorted([r for r in range(N) if r % 2 == p and r != c], key=lambda r: (r - c) % N)
    o, s = turn(1 - c % 2), turn(c % 2)
    return [o[0], s[0], o[1], s[1], o[2]]


def left(r, h):
    return (r % 2 == 0) == (h == 0)


def own(r, h):
    return (64, 1) if left(r, h) else (768, 0)


def place(r, h, q):
    return (q - r - 1) % N if left(r, h) else (q - r) % N


def lands(r, h):
    return (0, 320) if left(r, h) else (128, 0)


def build(topo, cores, E):
    ops = []
    now = [0]
    got = {}
    sent = {}
    arr = []
    R = range(N)

    def op(c, q, dur, deps, emit, kind="c", sem=None, lat=0.0):
        ops.append({"c": c, "q": q, "dur": dur, "deps": [d for d in deps if d is not None], "emit": emit, "kind": kind,
                    "sem": sem, "lat": lat, "bias": E["bias"] * now[0]})
        return len(ops) - 1

    def V(c, n, deps, emit, fast=False):
        return op(c, "V", max(64, n * (0.5 if fast else 1)) * E["v"], deps, emit)

    def S(c, n, deps, emit):
        return op(c, "S", E["s0"] + max(64, n) * E["s"], deps, emit)

    def X(c, n, deps, ev, es, ind=False):
        i = op(c, "V", 0.0, deps, None)
        dv, ds = max(64, n) * E["v"], E["s0"] + max(64, n) * E["s"]
        if ind:
            dv, ds = 0.05 + n * E["sg"], 0.065 + n * E["sg"]
        ops[i]["alt"] = {"V": (dv, ev), "S": (ds, es)}
        return i

    def G(c, n, deps, emit):
        return op(c, "G", E["g0"] + n * E["g"], deps, emit)

    def MM(c, n, deps, emit):
        return op(c, "P", (n + 16) * E["mm"], deps, emit)

    def D(c, q, deps, emit, sem, total=16, more=0.0):
        return op(c, q, E["dmai"], deps, emit, "d", (sem, total), E["dma"] + more)

    def QZ(c, n, deps, emit):
        return op(c, "V", 0.015 + 4 * n * 0.00034 * E["v"] / 0.001, deps, emit)

    def send(c, parts, deps):
        share = 1
        while share < len(parts):
            share *= 2

        def emit(g, T):
            ts = []
            for i, (dst, sem, src, land) in enumerate(parts):
                eng = topo.engines(cores[c], cores[dst[0]])
                w = len(eng) // share
                m = 0
                for e in eng[i * w:(i + 1) * w]:
                    m |= 1 << e
                ids = []
                for d in dst:
                    rid, pid, _ = topo.addr(cores[d])
                    ids.append(DstId(rid=rid, pnc=pid))
                ts.append(RemoteDMATransfer(dst_ids=ids, dma_engine_mask=m, remote_sem=T.sem[sem], srcs=[src(T)], dsts=[land(T, d) for d in dst], alu_op=0))
            return g.remote_dma_fused(ts, local_sem=T.sem.sent)
        for dst, sem, _, _ in parts:
            w = len(topo.engines(cores[c], cores[dst[0]])) // share
            for d in dst:
                got[(d, sem)] = got.get((d, sem), 0) + w
            sent[c] = sent.get(c, 0) + w
        return op(c, "G", E["rem"] + 0.06 * (len(parts) - 1), deps, emit, "r")

    def arrive(c, sem, deps, lat):
        o = op(c, None, 0.0, deps, None, "a", (sem, None), lat)
        arr.append(o)
        return o

    st = [{} for _ in R]
    for c in R:
        s = st[c]
        s["ldx"] = D(c, "Y", [], lambda g, T: g.sync.dma_start(T.xt[:], T.x[:]), "ld_x")
        s["ldc1"] = D(c, "Y", [], lambda g, T: g.sync.dma_start(T.ct1[:], T.c1[:]), "ld_c1", 16, 1.2)
        s["qx1"] = [QZ(c, 128, [s["ldx"]], lambda g, T, a=a: g.vector.quantize_mx(T.xq1[:, a:a + 128], T.xp1[:, a:a + 128], T.xt[:])) for a in (0, 768)]
        s["neg"] = V(c, 512, [], lambda g, T: g.vector.memset(T.neg[:], -1e29))
        s["ones"] = V(c, 516, [], lambda g, T: g.vector.memset(T.ones[:], 1.0), True)
        pi = G(c, 1, [], lambda g, T: g.iota(T.pi[:, 0:1], [[0, 1]], 0, 1))
        bm = G(c, 32, [], lambda g, T: g.iota(T.bm[:], [[0, 2], [1, 4], [0, 4]], 0, 0, allow_small_or_imprecise_dtypes=True))
        p3 = V(c, 1, [pi], lambda g, T: g.vector.tensor_scalar(T.p3[:, 0:1], T.pi[:, 0:1], 3, None, A.bitwise_and))
        s["acol"] = V(c, 1, [p3], lambda g, T: g.vector.tensor_copy(T.acol[:, 0:1], T.p3[:, 0:1]))
        s["mask"] = V(c, 32, [bm, s["acol"]], lambda g, T: g.vector.tensor_scalar(T.mask[:], T.bm[:], T.acol[:, 0:1], None, A.is_equal))
        s["aw"] = V(c, 1, [s["acol"]], lambda g, T: g.vector.tensor_scalar(T.aw[:, 0:1], T.acol[:, 0:1], float(CW), None, A.mult))
        s["qc1"] = QZ(c, 512, [s["ldc1"]], lambda g, T: g.vector.quantize_mx(T.cq1[:], T.cp1[:], T.ct1[:]))

    def spread(c, stage, h, q):
        dst = [(c + i) % N for i in range(1, N)]
        if h is None:
            sem, a, n, k = "xa1_%d" % c, 0, 128, 0
        else:
            sem, n = "xa2_%d_%d" % (h, c), 64
            a, k = own(c, h)
        to = lambda d: 128 + 128 * chain(d).index(c) + 64 * k
        s1 = send(c, [(dst, sem, lambda T: T["xq%d" % stage][:, a:a + n].bitcast(dt.uint8), lambda T, d: T["xq%d" % stage][:, to(d):to(d) + n].bitcast(dt.uint8))], [q])
        s2 = send(c, [(dst, sem, lambda T: T["xp%d" % stage][:, a:a + n], lambda T, d: T["xp%d" % stage][:, to(d):to(d) + n])], [q])
        for d in dst:
            o = arrive(d, sem, [s1, s2], E["hopx"] if h is None else E["hopr"])
            for e in ((0, 1) if h is None else (h,)):
                st[d]["x%d_%d_%d" % (stage, e, c)] = o

    for c in R:
        s = st[c]
        spread(c, 1, None, s["qx1"][0])
        for h in range(2):
            s["x1_%d_%d" % (h, c)] = s["qx1"][0 if left(c, h) else 1]
        s["zt"] = G(c, 516, [s["ones"]], lambda g, T: g.affine_select(T.zt[:], T.ones[:], [[-1, 516]], A.is_equal, 0.0, 4, 4))
        late = [s["qx1"][0]]
        s["wt"] = G(c, 6, late, lambda g, T: g.iota(T.wt[:, 0:N], [[-1, N]], 8, 0, allow_small_or_imprecise_dtypes=True))
        for h in range(2):
            m = min(c + 1, N - 1) if left(c, h) else max(c, 1)
            s["sl%d" % h] = [G(c, z - a, late, lambda g, T, h=h, a=a, z=z, b=64 * place(c, h, a) - (0 if left(c, h) else 64): g.iota(
                T.sl[:, 8 * h + a:8 * h + z], [[64, z - a]], b, 1, allow_small_or_imprecise_dtypes=True)) for a, z in ((0, m), (m, N))]
        s["q512"] = G(c, 6, late, lambda g, T: g.iota(T.q512[:, 0:N], [[K, N]], 0, 0, allow_small_or_imprecise_dtypes=True))
        s["eq"] = [QZ(c, 128, [s["zt"]], lambda g, T, b=b: g.vector.quantize_mx(T.eq[:, 128 * b:128 * b + 128], T.ep[:, 128 * b:128 * b + 128], T.zt[:, 4 - b:516 - b])) for b in range(4)]
        s["z"] = [V(c, 256, [], lambda g, T, h=h, z=(0 if left(c, h) else 256): g.vector.memset(T["rt%d" % h][:, z:z + 256], 0.0), True) for h in range(2)]
        s["ldc2"] = D(c, "Y", [s["qc1"]], lambda g, T: g.sync.dma_start(T.ct2[:], T.c2[:]), "ld_c2", 16, 1.5)
        s["qc2"] = QZ(c, 512, [s["ldc2"]], lambda g, T: g.vector.quantize_mx(T.cq2[:], T.cp2[:], T.ct2[:]))

    def spread_out(c, i, n, p, vals, deps):
        sl = i if n == 1 else slice(i, i + n)
        tr = []
        for k in range(n):
            m = X(c, 32, [deps[k], st[c]["mask"]], lambda g, T, k=k: g.vector.tensor_scalar(T.lx[p, i + k, :], T.mask[p, :], vals[k](T), None, A.mult),
                  lambda g, T, k=k: g.scalar.activation(T.lx[p, i + k, :], T.mask[p, :], F.Copy, scale=vals[k](T)))
            tr.append(V(c, 32, [m], lambda g, T, k=k: g.vector.transpose(T.lt[p, i + k, :], T.lx[p, i + k, :])))
        y = V(c, 32 * n, tr, lambda g, T: g.vector.tensor_tensor(T.ly[p, sl, :], T.lt[p, sl, 0::2], T.lt[p, sl, 1::2], A.add))
        return V(c, 16 * n, [y], lambda g, T: g.vector.tensor_tensor(T.lz[p, sl, :], T.ly[p, sl, 0::2], T.ly[p, sl, 1::2], A.add))

    def word_list(c, i, n, vals, deps):
        sl = slice(i, i + n)
        z = spread_out(c, i, n, slice(0, 128), vals, deps)
        half = []
        for d in range(2):
            for b in range(2):
                for a in range(2):
                    o, f = slice(64 * d + 32 * b, 64 * d + 32 * b + 32), slice(64 * d + 32 * a, 64 * d + 32 * a + 32)
                    half.append(X(c, 8 * n, [z], lambda g, T, o=o, f=f, a=a: g.vector.tensor_copy(T.ls[o, sl, 8 * a:8 * a + 8], T.lz[f, sl, :]),
                                  lambda g, T, o=o, f=f, a=a: g.scalar.activation(T.ls[o, sl, 8 * a:8 * a + 8], T.lz[f, sl, :], F.Copy)))
        out = []
        for h in range(2):
            for d in range(2):
                o, f = slice(64 * d, 64 * d + 64), slice(64 * h, 64 * h + 64)
                out.append(V(c, 16 * n, half[4 * h:4 * h + 4] + [st[c]["acol"]], lambda g, T, o=o, f=f, h=h: g.vector.tensor_scalar(
                    T.off[o, sl, 16 * h:16 * h + 16], T.ls[f, sl, :], 4.0, T.acol[f, 0:1], A.mult, A.add)))
        return out

    scans = [[] for _ in R]
    slot = [0] * N
    pairs = {(s, h): [[] for _ in R] for s in (1, 2) for h in range(2)}
    cands = {(s, h): [[] for _ in R] for s in (1, 2) for h in range(2)}

    def search(c, stage, h):
        s = st[c]
        ch = chain(c)
        ot = lands(c, h)[1]
        tiles = [(192, (ch[0], ch[1])), (448, (ch[2], ch[3])), (704, (ch[4], c))]
        if left(c, h):
            tiles = [(320, (ch[1], ch[2])), (576, (ch[3], ch[4])), (64, (c, ch[0]))]
        seq = [2, 0, 1]
        nm = lambda k: "%d_%d_%d" % (stage, h, k)
        wq, wp, sc_ = "wq%d_%d" % (stage, h), "wp%d_%d" % (stage, h), "sc%d_%d" % (stage, h)
        sg = {}
        for k in seq:
            col, who = tiles[k]
            bank = len(scans[c]) % 4
            prev = scans[c][-4] if len(scans[c]) >= 4 else None
            m = MM(c, 512, [s["x%d_%d_%d" % (stage, h, r)] for r in who] + [s["qc%d" % stage], prev], lambda g, T, col=col, bank=bank: g.tensor.matmul_mx(
                T.sb[:, 512 * bank:512 * bank + 512], T["xq%d" % stage][:, col:col + 128], T["xp%d" % stage][:, col:col + 128], T["cq%d" % stage][:], T["cp%d" % stage][:], True, True))
            sc = V(c, 512, [m, s["neg"]], lambda g, T, k=k, bank=bank: g.vector.tensor_tensor_scan(
                T["rm" + nm(k)][:, 0:512], T.sb[:, 512 * bank:512 * bank + 512], T.neg[:], -1e29, A.max, A.max))
            scans[c].append(sc)
            sg[k] = S(c, 512, [sc], lambda g, T, k=k: g.scalar.activation(
                T["jk" + nm(k)][:], T["rm" + nm(k)][:, 0:512], F.Sign, bias=T["rm" + nm(k)][:, 511:512], scale=-1.0, accum_out=T["rm" + nm(k)][:, 512:513]))
        o = send(c, [([r for r in tiles[k][1] if r != c], "pair%d_%d" % (stage, h), lambda T, k=k: T["rm" + nm(k)][:, 511:513],
                      lambda T, d: T[sc_][:, 4 * c:4 * c + 2]) for k in range(3)], [sg[k] for k in range(3)])
        for r in R:
            if r != c:
                pairs[(stage, h)][r].append(o)
        pb = slice(0, 64) if left(c, h) else slice(64, 128)
        s["own%d_%d" % (stage, h)] = V(c, 2, [sg[2]], lambda g, T: g.vector.tensor_copy(T[sc_][pb, 4 * c:4 * c + 2], T["rm" + nm(2)][pb, 511:513]))
        i0 = slot[c]
        slot[c] += 3
        ls = word_list(c, i0, 3, [lambda T, k=k: T["rm" + nm(k)][:, 512:513] for k in seq], [sg[k] for k in seq])
        qs = {}
        for j, k in enumerate(seq):
            i = i0 + j
            ga = [X(c, 256, ls,
                    lambda g, T, k=k, i=i, e=e: g.vector.tensor_copy(T["gt" + nm(k)][:, 256 * e:256 * e + 256], T["ct%d" % stage][:, 0:4 * K].indirect(T.off[:, i, 16 * e:16 * e + 16])),
                    lambda g, T, k=k, i=i, e=e: g.scalar.activation(T["gt" + nm(k)][:, 256 * e:256 * e + 256], T["ct%d" % stage][:, 0:4 * K].indirect(T.off[:, i, 16 * e:16 * e + 16]), F.Copy), True) for e in range(2)]
            if k == 2:
                qs[k] = QZ(c, 128, ga, lambda g, T: g.vector.quantize_mx(T[wq][:, ot:ot + 128], T[wp][:, ot:ot + 128], T["gt" + nm(2)][:]))
                s["w%d_%d" % (stage, h)] = qs[k]
            else:
                qs[k] = QZ(c, 128, ga, lambda g, T, k=k: g.vector.quantize_mx(T["oq" + nm(k)][:], T["op" + nm(k)][:], T["gt" + nm(k)][:]))
        sem = "wa%d_%d" % (stage, h)
        to = lambda d: lands(d, h)[0] + 64 * ((c - d - 1) % N)
        for part in ([2], [0, 1]):
            pc, pp = [], []
            for k in part:
                for e, r in enumerate(tiles[k][1]):
                    if r != c:
                        a, bq, bp = (ot + 64 * e, wq, wp) if k == 2 else (64 * e, "oq" + nm(k), "op" + nm(k))
                        pc.append(([r], sem, lambda T, bq=bq, a=a: T[bq][:, a:a + 64].bitcast(dt.uint8), lambda T, d: T[wq][:, to(d):to(d) + 64].bitcast(dt.uint8)))
                        pp.append(([r], sem, lambda T, bp=bp, a=a: T[bp][:, a:a + 64], lambda T, d: T[wp][:, to(d):to(d) + 64]))
            s1 = send(c, pc, [qs[k] for k in part])
            s2 = send(c, pp, [qs[k] for k in part])
            for p in pc:
                cands[(stage, h)][p[0][0]] += [s1, s2]

    upd = [{} for _ in R]
    joint = [{} for _ in R]

    def finish(c, stage, h):
        s = st[c]
        dc, sc, win = "dc%d" % stage, "sc%d_%d" % (stage, h), "win%d_%d" % (stage, h)
        pb = slice(0, 64) if left(c, h) else slice(64, 128)
        p0 = 0 if left(c, h) else 64
        p1 = 64 - p0
        pa = arrive(c, "pair%d_%d" % (stage, h), pairs[(stage, h)][c], E["hop"])
        wa = arrive(c, "wa%d_%d" % (stage, h), cands[(stage, h)][c], E["hop"])
        col = lambda T, k: T[dc][pb, k:k + 1]
        ow = s["own%d_%d" % (stage, h)]
        m = V(c, 6, [pa, ow], lambda g, T: g.vector.tensor_reduce(col(T, 0), T[sc][pb, 0::4], AxisListType.X, A.max))
        e = V(c, 6, [m], lambda g, T: g.vector.tensor_scalar(T[dc][pb, 8:8 + N], T[sc][pb, 0::4], col(T, 0), None, A.is_equal))
        w = V(c, 6, [e, s["wt"]], lambda g, T: g.vector.tensor_tensor(T[dc][pb, 16:16 + N], T[dc][pb, 8:8 + N], T.wt[pb, 0:N], A.mult))
        k8 = V(c, 6, [w], lambda g, T: g.vector.tensor_reduce(col(T, 1), T[dc][pb, 16:16 + N], AxisListType.X, A.max))
        oh = V(c, 6, [k8], lambda g, T: g.vector.tensor_scalar(T[dc][pb, 24:24 + N], T[dc][pb, 16:16 + N], col(T, 1), None, A.is_equal))
        pv = V(c, 6, [oh] + s["sl%d" % h], lambda g, T: g.vector.tensor_tensor(T[dc][pb, 40:40 + N], T[dc][pb, 24:24 + N], T.sl[pb, 8 * h:8 * h + N], A.mult))
        v = V(c, 6, [pv], lambda g, T: g.vector.tensor_reduce(col(T, 2), T[dc][pb, 40:40 + N], AxisListType.X, A.add))
        i = slot[c]
        slot[c] += 1
        z = spread_out(c, i, 1, pb, [lambda T: col(T, 2)], [v])
        near = []
        for b in range(2):
            for a in range(2):
                o, f = slice(p0 + 32 * b, p0 + 32 * b + 32), slice(p0 + 32 * a, p0 + 32 * a + 32)
                near.append(V(c, 8, [z, s["aw"]], lambda g, T, o=o, f=f, a=a: g.vector.tensor_scalar(T.off[o, i, 8 * a:8 * a + 8], T.lz[f, i, :], 1.0, T.aw[f, 0:1], A.mult, A.add)))
        ls = [V(c, 16, near, lambda g, T: g.vector.tensor_copy(T.off[p1:p1 + 64, i, 0:16], T.off[pb, i, 0:16]))]
        gn = V(c, 6, [pa, ow, s["q512"]], lambda g, T: g.vector.tensor_tensor(T[dc][pb, 32:32 + N], T[sc][pb, 1::4], T.q512[pb, 0:N], A.add))
        joint[c].setdefault(stage, []).extend([m, oh, gn])
        of, ot = lands(c, h)
        cps = []
        for mine in (True, False):
            for b in range(4):
                a, n = (ot, 128) if mine else (of, 320)
                f, k, o = (p0, 64, 64 * place(c, h, c)) if mine else (0, 320, 64 * place(c, h, (c + 1) % N))
                u = MM(c, n, [s["w%d_%d" % (stage, h)] if mine else wa, s["eq"][b], upd[c].get(b)], lambda g, T, b=b, a=a, n=n: g.tensor.matmul_mx(
                    T.up[:, 512 * b:512 * b + n], T.eq[:, 128 * b:128 * b + 128], T.ep[:, 128 * b:128 * b + 128],
                    T["wq%d_%d" % (stage, h)][:, a:a + n], T["wp%d_%d" % (stage, h)][:, a:a + n], True, True))
                to = lambda T, b=b, o=o, k=k: T[win][:, CW * b + o:CW * b + o + k]
                fr = lambda T, b=b, f=f, k=k: T.up[:, 512 * b + f:512 * b + f + k]
                cp = X(c, k, [u], lambda g, T, to=to, fr=fr: g.vector.tensor_scalar(to(T), fr(T), -1.0, None, A.mult),
                       lambda g, T, to=to, fr=fr: g.scalar.activation(to(T), fr(T), F.Copy, scale=-1.0))
                upd[c][b] = cp
                cps.append(cp)
        half = 1 if left(c, h) else 0
        if stage == 1:
            r = V(c, 450, cps + ls + s["z"] + [s["ldx"]], lambda g, T: g.vector.tensor_tensor(
                T["rt%d" % h][:, 256 * half:256 * half + 256], T[win][:, 0:4 * CW].indirect(T.off[:, i, 0:16]), T.xt[:, 256 * half:256 * half + 256], A.add))
            s["r%d" % h] = r
            a = 0 if left(c, h) else 768
            q2 = QZ(c, 128, [r], lambda g, T: g.vector.quantize_mx(T.xq2[:, a:a + 128], T.xp2[:, a:a + 128], T["rt%d" % h][:]))
            s["x2_%d_%d" % (h, c)] = q2
            spread(c, 2, h, q2)
        else:
            for k in range(2):
                y = V(c, 225, cps + ls + [s["r%d" % h]], lambda g, T, k=k: g.vector.tensor_tensor(
                    T["yt%d" % h][:, 128 * k:128 * k + 128], T[win][:, 0:4 * CW].indirect(T.off[:, i, 8 * k:8 * k + 8]), T["rt%d" % h][:, 256 * half + 128 * k:256 * half + 128 * k + 128], A.add))
                a = 256 * half + 128 * k
                if k == 0:
                    D(c, "Y", [y], lambda g, T, a=a, k=k: g.sync.dma_start(T.y[:, a:a + 128], T["yt%d" % h][:, 128 * k:128 * k + 128]), "st_y%d_%d" % (k, h))
                else:
                    D(c, "S", [y], lambda g, T, a=a, k=k: g.scalar.dma_start(T.y[:, a:a + 128], T["yt%d" % h][:, 128 * k:128 * k + 128]), "st_y%d_%d" % (k, h))

    def numbers(c, stage):
        dc = "dc%d" % stage
        d = joint[c][stage]
        pr = V(c, 6, d, lambda g, T: g.vector.tensor_tensor(T[dc][:, 48:48 + N], T[dc][:, 24:24 + N], T[dc][:, 32:32 + N], A.mult))
        nu = V(c, 6, [pr], lambda g, T: g.vector.tensor_reduce(T[dc][:, 3:4], T[dc][:, 48:48 + N], AxisListType.X, A.add))
        for row, cc in ((stage - 1, 3), (stage + 1, 0)):
            for h in range(2):
                f, o = (0, 64) if left(c, h) else (64, 0)
                D(c, "Y", [nu] if cc == 3 else d, lambda g, T, row=row, cc=cc, f=f, o=o: g.sync.dma_start(T.no[row:row + 1, o:o + 64], T[dc][f:f + 64, cc:cc + 1]), "st_no", 128)

    for stage in (1, 2):
        for h in range(2):
            now[0] = h if stage == 1 else 1 + h
            for c in R:
                search(c, stage, h)
            for c in R:
                finish(c, stage, h)
        for c in R:
            numbers(c, stage)
    for o in arr:
        ops[o]["sem"] = (ops[o]["sem"][0], got[(ops[o]["c"], ops[o]["sem"][0])])
    return ops, sent


def alike(ops):
    per = [[i for i, o in enumerate(ops) if o["c"] == c and o["kind"] != "a"] for c in range(N)]
    calls = [[i for i in l if ops[i]["kind"] == "r"] for l in per]
    back = {}
    for l in calls:
        for k, i in enumerate(l):
            back[i] = calls[LEAD][k]
    ids = per[LEAD] + [i for i, o in enumerate(ops) if o["c"] == LEAD and o["kind"] == "a"]
    at = {i: k for k, i in enumerate(ids)}
    return per, ids, [sorted(set(at[back.get(d, d)] for d in ops[i]["deps"])) for i in ids]


def draw_up(topo, cores):
    ops, sent = build(topo, cores, SETS[0])
    per, ids, deps = alike(ops)
    n = len(ids)
    R = range(n)
    sets = []
    for E in SETS:
        full = build(topo, cores, E)[0]
        lead = [full[i] for i in ids]
        sets.append(([{q: v[0] for q, v in o["alt"].items()} if "alt" in o else {o["q"]: o["dur"]} for o in lead], [o["lat"] for o in lead], E["wake"]))
    lead = [ops[i] for i in ids]
    alt = ["alt" in o for o in lead]
    home = [o["q"] for o in lead]
    succ = [[] for _ in R]
    for i in R:
        for d in deps[i]:
            succ[d].append(i)
    cnt = [len(d) for d in deps]
    top = [i for i in R if cnt[i] == 0]
    for i in top:
        for j in succ[i]:
            cnt[j] -= 1
            if cnt[j] == 0:
                top.append(j)
    rank = [0.0] * n
    for j in reversed(top):
        rank[j] = min(sets[0][0][j].values()) + sets[0][1][j] + sets[0][2] + max([rank[k] for k in succ[j]] + [0.0])
    rank = [rank[i] - lead[i]["bias"] for i in R]

    def order(nudge, pin, favour):
        dur, lat, wake = sets[0]
        todo = [len(d) for d in deps]
        at = [0.0] * n
        ready = {q: [] for q in ("V", "S", "P", "G", "Y", None)}
        free = {q: 0.0 for q in ready}
        seq = {q: [] for q in ready}
        qof = [None] * n
        pr = [rank[i] + nudge[i] for i in R]

        def add(i):
            if not alt[i]:
                ready[home[i]].append(i)
                return
            for q in ("V", "S"):
                if pin[i] in (None, q):
                    ready[q].append(i)
        for i in R:
            if todo[i] == 0:
                add(i)
        for _ in R:
            bt, bq = 1e9, None
            for q, l in ready.items():
                if l:
                    t = min([at[i] for i in l])
                    if q and free[q] > t:
                        t = free[q]
                    if t < bt:
                        bt, bq = t, q
            i, bp = -1, -1e9
            for j in ready[bq]:
                if at[j] <= bt:
                    p = pr[j] - (favour if bq == "V" and alt[j] else 0.0)
                    if p > bp:
                        i, bp = j, p
            ready[bq].remove(i)
            if alt[i]:
                o = "S" if bq == "V" else "V"
                if i in ready[o]:
                    ready[o].remove(i)
            qof[i] = bq
            e = bt + dur[i][bq]
            if bq:
                free[bq] = e
            seq[bq].append(i)
            for k in succ[i]:
                todo[k] -= 1
                at[k] = max(at[k], e + lat[i] + (0.06 if bq == home[k] and not alt[k] else wake))
                if todo[k] == 0:
                    add(k)
        return seq, qof

    def span(seq, qof, which):
        dur, lat, wake = sets[which]
        todo = [len(d) for d in deps]
        at = [0.0] * n
        pos = {q: 0 for q in seq}
        free = {q: 0.0 for q in seq}
        end = 0.0
        land = [i for i in R if qof[i] is None and todo[i] == 0]
        moved = True
        while moved:
            moved = False
            for q, l in seq.items():
                while (land if q is None else pos[q] < len(l) and todo[l[pos[q]]] == 0):
                    i = land.pop() if q is None else l[pos[q]]
                    pos[q] += 1
                    e = at[i] if q is None else max(at[i], free[q]) + dur[i][q]
                    free[q] = e
                    moved = True
                    d = e + lat[i]
                    if d > end:
                        end = d
                    for k in succ[i]:
                        todo[k] -= 1
                        a = d + (0.06 if q and qof[k] == q else wake)
                        if a > at[k]:
                            at[k] = a
                        if todo[k] == 0 and qof[k] is None:
                            land.append(k)
        return end

    seed = [12345]

    def draw(m):
        seed[0] = (seed[0] * 1103515245 + 12345) % (1 << 31)
        return (seed[0] >> 8) % m

    work = [i for i in R if home[i] in ("V", "S")]
    both = [i for i in work if alt[i]]
    cur = ([0.0] * n, [None] * n, 1.0)
    kept = order(*cur)
    base = [span(kept[0], kept[1], k) for k in range(len(SETS))]
    now = best = 1.0
    for step in range(STEPS):
        nudge, pin, favour = list(cur[0]), list(cur[1]), cur[2]
        k = draw(100)
        if k < 60:
            for _ in range(1 + draw(3)):
                nudge[work[draw(len(work))]] = (draw(61) - 30) / 10.0 if draw(10) < 7 else 0.0
        elif k < 75:
            a, d = draw(len(work)), (draw(51) - 25) / 10.0
            for i in work[a:a + 3 + draw(38)]:
                nudge[i] += d
        elif k < 97:
            for _ in range(1 + draw(3)):
                pin[both[draw(len(both))]] = (None, "V", "S")[draw(3)]
        else:
            favour = (0.0, 0.5, 1.0, 1.5, 2.0, 3.0)[draw(6)]
        so = order(nudge, pin, favour)
        v = sum(span(so[0], so[1], k) / base[k] for k in range(len(SETS))) / len(SETS)
        if v <= now + 0.003 * max(0.0, 1.0 - step / (0.9 * STEPS)) * draw(1000) / 1000.0:
            cur, now = (nudge, pin, favour), v
            if v < best:
                best, kept = v, so
    seq = {}
    for c in range(N):
        for q, l in kept[0].items():
            if q:
                seq[(c, q)] = [per[c][k] for k in l]
        for k in both:
            o = ops[per[c][k]]
            o["q"] = kept[1][k]
            o["emit"] = o["alt"][o["q"]][1]
    return ops, sent, seq, [span(kept[0], kept[1], k) for k in range(len(SETS))]


def plan(topo, cores):
    if "plan" not in _memo:
        _memo["plan"] = draw_up(topo, cores)
    return _memo["plan"]


def rank_program(g, core, T, topo):
    rank = T.rank_of(core)
    if rank is None:
        return
    ops, sent, seq, _ = plan(topo, list(T.cores))
    queues = {"V": g.vector, "S": g.scalar, "P": g.tensor, "G": g, "Y": g.sync}
    num = {}
    tot = {"sent": sent[rank]}
    for q in CSEM:
        k = 0
        for i in seq.get((rank, q), []):
            if ops[i]["kind"] == "c":
                k += 1
                num[i] = (CSEM[q], k)
        tot[CSEM[q]] = k
    known = {q: {} for q in queues}
    snap = {}
    pos = {q: 0 for q in queues}
    mine = sum(len(seq.get((rank, q), [])) for q in queues)
    while mine:
        moved = False
        for q in queues:
            lst = seq.get((rank, q), [])
            while pos[q] < len(lst) and all(ops[d]["kind"] in "ra" or d in snap for d in ops[lst[pos[q]]]["deps"]):
                i = lst[pos[q]]
                o = ops[i]
                need = {}
                for d in o["deps"]:
                    name, cnt = num[d] if ops[d]["kind"] == "c" else ops[d]["sem"]
                    if need.get(name, (0, None))[0] < cnt:
                        need[name] = (cnt, snap.get(d))
                for name in sorted(need, key=lambda t: -len(need[t][1] or {})):
                    cnt, sn = need[name]
                    if known[q].get(name, 0) < cnt:
                        queues[q].wait_ge(T.sem[name], cnt)
                        known[q][name] = cnt
                        for k2, v2 in (sn or {}).items():
                            known[q][k2] = max(known[q].get(k2, 0), v2)
                ins = o["emit"](g, T)
                if o["kind"] == "c":
                    ins.then_inc(T.sem[num[i][0]], 1)
                elif o["kind"] == "d":
                    ins.then_inc(T.sem[o["sem"][0]], 16)
                snap[i] = dict(known[q])
                pos[q] += 1
                mine -= 1
                moved = True
        if not moved:
            raise ValueError("the plan does not close")
    for o in ops:
        if o["c"] == rank and o["kind"] in "da":
            tot[o["sem"][0]] = o["sem"][1]
    for name in SEMAPHORES:
        if tot.get(name, 0) > known["G"].get(name, 0):
            g.wait_ge(T.sem[name], tot[name])
